import numpy as np
import ml_dtypes


def mxq(x, axis, fmt="e4m3"):
    dtype, down = {"e4m3": (ml_dtypes.float8_e4m3fn, 7), "e5m2": (ml_dtypes.float8_e5m2, 14)}[fmt]
    v = np.moveaxis(np.asarray(x, np.float32).astype(ml_dtypes.bfloat16).astype(np.float64), axis, -1)
    blocks = v.reshape(v.shape[:-1] + (-1, 32))
    amax = np.abs(blocks).max(-1, keepdims=True)
    byte = np.maximum(np.where(amax > 0, np.frexp(amax)[1] - 1 + 127, 0) - down, 1)
    scale = np.exp2(byte - 127.0)
    codes = (blocks / scale).astype(np.float32).astype(dtype).astype(np.float64)
    return np.moveaxis((codes * scale).reshape(v.shape), -1, axis)


WIDE = False


def mx_kscale(k):
    if not WIDE:
        return np.ones(k)
    levels = np.array([10, -10, 5, -5, 0])
    if k % 512:
        return np.exp2(np.random.permutation(np.resize(levels, k // 32))).repeat(32)
    a = np.empty((k // 512, 16))
    for p in range(k // 512):
        a[p, :8] = np.random.permutation(np.resize(levels, 8))
        for g in range(8):
            far = levels[np.abs(levels - a[p, g]) >= 10]
            a[p, g + 8] = far[np.random.randint(len(far))]
    return np.exp2(a.ravel()).repeat(32)


def f64(x):
    return np.asarray(x).astype(np.float64)


def striped(idx):
    return np.tile(idx.reshape(-1, 16).T, (8, 1)).astype(np.uint16)


def unstriped(offs):
    return offs[:16].T.reshape(-1).astype(np.int64)


E2M1 = np.array([0.0, 0.5, 1.0, 1.5, 2.0, 3.0, 4.0, 6.0, -0.0, -0.5, -1.0, -1.5, -2.0, -3.0, -4.0, -6.0])


def pack_weight(w, fmt):
    k, n = w.shape
    w = f64(np.asarray(w, np.float32).astype(ml_dtypes.bfloat16)).reshape(k // 32, 32, n)
    amax = np.abs(w).max(1)
    if fmt == "e4m3":
        byte = np.frexp(amax)[1] - 1 + 127 - 7
    else:
        mant, ex = np.frexp(amax / 6.0)
        byte = np.where(mant > 0.5, ex, ex - 1) + 127
    byte = np.clip(np.where(amax > 0, byte, 1), 1, 254)
    scaled = (w * np.exp2(127.0 - byte)[:, None, :]).reshape(k, n).astype(np.float32)
    by_word = np.ascontiguousarray(scaled.reshape(k // 512, 128, 4, n).transpose(0, 1, 3, 2))
    if fmt == "e4m3":
        words = by_word.astype(ml_dtypes.float8_e4m3fn).view(np.uint8)
    else:
        c = by_word.astype(ml_dtypes.float4_e2m1fn).view(np.uint8) & 0xF
        words = (c[..., 0::2] | (c[..., 1::2] << 4)).reshape(k // 512, 128, 2 * n)
    return np.ascontiguousarray(words), np.ascontiguousarray(byte.astype(np.uint8).reshape(k // 512, 16, n))


def unpack_weight(words, scales, fmt):
    g, _, n = scales.shape
    words = np.ascontiguousarray(words).reshape(g, 128, n, -1)
    if fmt == "e4m3":
        vals = words.view(ml_dtypes.float8_e4m3fn).astype(np.float64)
    else:
        nib = np.empty((g, 128, n, 4), np.uint8)
        nib[..., 0::2] = words & 0xF
        nib[..., 1::2] = words >> 4
        vals = E2M1[nib]
    vals = vals * np.repeat(np.exp2(scales.astype(np.float64) - 127.0), 8, axis=1)[..., None]
    return vals.transpose(0, 1, 3, 2).reshape(g * 512, n)


def gelu(v):
    return 0.5 * v * (1.0 + np.tanh(np.sqrt(2.0 / np.pi) * (v + 0.044715 * v**3)))


K, T, S, H, T2, P = 1536, 2048, 512, 1024, 1024, 512

def setup_inputs():
    n = np.random.standard_normal
    s = mx_kscale(K)[:, None]
    u = mx_kscale(H)[:, None]
    d = {}
    d["tab_words"], d["tab_scales"] = pack_weight(n((K, T)) * s, "e4m3")
    d["offs"] = striped(np.random.permutation(T)[:S])
    d["offs2"] = striped(np.random.permutation(T2)[:S])
    d["offs3"] = striped(np.random.permutation(T2)[:P])
    d["w1"] = (1.5 * n((K, H)) / K**0.5 / s).astype(np.float32)
    d["w4_words"], d["w4_scales"] = pack_weight(1.5 * n((K, H)) / K**0.5 / s, "e2m1")
    d["gain"] = (np.exp(0.4 * n(H)) * u[:, 0]).astype(np.float32)
    d["wgs"] = np.exp(0.3 * n((128, S))).astype(np.float32)
    d["page0"] = (1.2 * n((H, T2)) * u).astype(np.float32)
    d["marks"] = (n((H, P)) * u).astype(np.float32)
    d["rv"] = (n(H) / H**0.5 / u[:, 0]**2).astype(np.float32)
    d["slot"] = (0.7 * n(T2)).astype(np.float32)
    return d

def reference(tab_words, tab_scales, offs, offs2, offs3, w1, w4_words, w4_scales, gain, wgs, page0, marks, rv, slot):
    v = unpack_weight(tab_words, tab_scales, "e4m3")[:, unstriped(offs)]
    y1 = mxq(f64(w1), 0, "e4m3").T @ v
    y4 = unpack_weight(w4_words, w4_scales, "e2m1").T @ v
    t = np.tanh(np.vstack((y1, y4)))
    h = f64(gain)[:, None] * (t[:H] - t[H:])
    page = f64(page0).copy()
    page[:, unstriped(offs2)] = np.tile(f64(wgs), (H // 128, 1)) * h
    x = (page[:, unstriped(offs3)] + f64(marks)) * f64(rv)[:, None]
    e = mxq(page, 0, "e4m3").T @ mxq(x, 0, "e4m3")
    return np.abs(e) * f64(slot)[:, None]

@@ -1,0 +1,352 @@
+from contextlib import ExitStack
+
+import concourse.mybir as mybir
+from concourse.masks import make_identity
+
+K, T, S, H, T2, NP = 1536, 2048, 512, 1024, 1024, 512
+FLOPS = 2 * (2 * K * H * S + H * T2 * NP)
+
+F32 = mybir.dt.float32
+BF16 = mybir.dt.bfloat16
+U32 = mybir.dt.uint32
+I32 = mybir.dt.int32
+U16 = mybir.dt.uint16
+U8 = mybir.dt.uint8
+FP8X4 = mybir.dt.float8_e4m3fn_x4
+FP4X4 = mybir.dt.float4_e2m1fn_x4
+ALU = mybir.AluOpType
+ACT = mybir.ActivationFunctionType
+
+P = 128
+KP = 3
+RP = 2
+SCATTER_WIDTHS = [[128, 128, 256], [512]]
+X_WIDTHS = [[512], [256, 256]]
+OUT_WIDTHS = [256, 128, 128]
+
+
+def spans(widths):
+    starts = [sum(widths[:i]) for i in range(len(widths))]
+    return list(zip(starts, widths))
+
+
+def tile_list_ballot_mark_review_kernel(
+    tc, tab_words, tab_scales, offs, offs2, offs3, w1, w4_words, w4_scales, gain, wgs, page0, marks, rv, slot, out
+):
+    nc = tc.nc
+    with ExitStack() as ctx:
+        keep = ctx.enter_context(tc.tile_pool(name="keep", bufs=1))
+        psum = ctx.enter_context(tc.psum_pool(name="psum", bufs=8))
+
+        def tile(name, shape, dtype):
+            return keep.tile(shape, dtype, name=name, align_bytes=64)
+
+        idx = tile("idx", [P, S // 16], U16)
+        idx2 = tile("idx2", [P, S // 16], U16)
+        idx3 = tile("idx3", [P, NP // 16], U16)
+        ident = tile("ident", [P, P], F32)
+        gain4 = tile("gain4", [P, RP, 4], F32)
+        rv4 = tile("rv4", [P, RP, 4], F32)
+        slot8 = tile("slot8", [P, 8], F32)
+        tabw = [tile("tabw%d" % a, [P, T], U32) for a in range(KP)]
+        tabs = tile("tabs", [P, KP, T], U8)
+        vw = [tile("vw%d" % a, [P, S], U32) for a in range(KP)]
+        vs = [tile("vs%d" % a, [P, S], U8) for a in range(KP)]
+        raw = [tile("raw%d" % a, [P, 4, 512], F32) for a in range(KP)]
+        wi0 = tile("wi0", [P, 512, 4], BF16)
+        wi12 = tile("wi12", [P, 1024, 4], BF16)
+        wi = [wi0[:], wi12[:, 0:512, :], wi12[:, 512:1024, :]]
+        w1c = [tile("w1c%d" % b, [P, KP * 512], U32) for b in range(RP)]
+        w1s = [tile("w1s%d" % b, [P, KP * 512], U8) for b in range(RP)]
+        w4w = [tile("w4w%d" % b, [P, KP, 1024], U8) for b in range(RP)]
+        w4s = [tile("w4s%d" % b, [P, KP, 512], U8) for b in range(RP)]
+        wgs_rows = tile("wgs_rows", [P, S], F32)
+        factor = [tile("factor%d" % b, [P, 4, S], F32) for b in range(RP)]
+        page = [[tile("page%d%d" % (b, t), [P, T2], F32) for t in range(4)] for b in range(RP)]
+        marks4 = [tile("marks%d" % b, [P, 4, NP], F32) for b in range(RP)]
+        tt = [tile("tt%d" % s, [P, 4, 512], F32) for s in range(2)]
+        hs = [tile("hs%d" % b, [P, 4, S], F32) for b in range(RP)]
+        pi1 = tile("pi1", [P, 4096], BF16)
+        pi = [
+            [tt[0][:, 2 * mh : 2 * mh + 2, :].rearrange("p a c -> p (a c)").bitcast(BF16).rearrange("p (c t) -> p c t", t=4) for mh in range(2)],
+            [pi1[:, 2048 * mh : 2048 * (mh + 1)].rearrange("p (c t) -> p c t", t=4) for mh in range(2)],
+        ]
+        pc = [tile("pc%d" % b, [P, T2], U32) for b in range(RP)]
+        ps = [tile("ps%d" % b, [P, T2], U8) for b in range(RP)]
+        spare = raw[0][:].rearrange("p j c -> p (j c)").bitcast(BF16)
+        xp = spare[:, 0:2048].rearrange("p (t j) -> p t j", t=4)
+        xi0 = spare[:, 2048:4096].rearrange("p (j t) -> p j t", t=4)
+        xi1 = [tile("xi1%d" % c, [P, w, 4], BF16) for c, w in enumerate(X_WIDTHS[1])]
+        xc = [tile("xc%d" % b, [P, NP], U32) for b in range(RP)]
+        xs = [tile("xs%d" % b, [P, NP], U8) for b in range(RP)]
+
+        nc.gpsimd.memset(tabs[:, 0, :].bitcast(I32), 0)
+        nc.vector.memset(tabs[:, 1:KP, :].bitcast(I32), 0)
+        for b in range(RP):
+            nc.gpsimd.memset(w4s[b][:].bitcast(I32), 0)
+        make_identity(nc, ident[:])
+
+        def load_tab(a):
+            nc.sync.dma_start(out=tabw[a][:].bitcast(I32), in_=tab_words[a].rearrange("p t i -> p (t i)").bitcast(I32))
+
+        def load_w1(b, a):
+            rows = w1[512 * a : 512 * (a + 1), 512 * b : 512 * (b + 1)]
+            nc.sync.dma_start(out=raw[a][:], in_=rows.rearrange("(p j) c -> p j c", j=4))
+
+        def load_w4(b):
+            nc.sync.dma_start(
+                out=w4w[b][:].bitcast(I32),
+                in_=w4_words[:, :, 1024 * b : 1024 * (b + 1)].rearrange("a p c -> p a c").bitcast(I32),
+            )
+
+        def load_w4s(b):
+            for q in range(4):
+                nc.sync.dma_start(
+                    out=w4s[b][32 * q : 32 * q + 4, :, :].bitcast(I32),
+                    in_=w4_scales[:, 4 * q : 4 * q + 4, 512 * b : 512 * (b + 1)].rearrange("a r c -> r a c").bitcast(I32),
+                )
+
+        def load_page(b, t):
+            rows = page0[512 * b : 512 * (b + 1), :].rearrange("(p t) m -> p t m", t=4)
+            nc.sync.dma_start(out=page[b][t][:], in_=rows[:, t, :])
+
+        def load_marks(b):
+            nc.sync.dma_start(out=marks4[b][:], in_=marks[512 * b : 512 * (b + 1), :].rearrange("(p t) j -> p t j", t=4))
+
+        def weave(engine_copy, dst, src):
+            engine_copy(out=dst.rearrange("p (c i) t -> p c t i", i=4), in_=src.rearrange("p t (c i) -> p c t i", i=4))
+
+        def quantize(codes, scales, woven):
+            nc.vector.quantize_mx(out=codes.bitcast(FP8X4), scales=scales, in_=woven.rearrange("p c t -> p (c t)"))
+
+        def quant_w1(b, a):
+            weave(nc.scalar.copy, wi[a], raw[a][:])
+            if b == 0 or a == 0:
+                quantize(w1c[b][:, 512 * a : 512 * (a + 1)], w1s[b][:, 512 * a : 512 * (a + 1)], wi[a])
+            elif a == 2:
+                quantize(w1c[b][:, 512:1536], w1s[b][:, 512:1536], wi12[:])
+
+        def gather_tab(a, pieces):
+            w = S // pieces
+            for i in range(pieces):
+                nc.vector.tensor_copy(
+                    out=vw[a][:, w * i : w * (i + 1)], in_=tabw[a][:].indirect(idx[:, w * i // 16 : w * (i + 1) // 16])
+                )
+
+        def mm_first(bank, term, b, a, jb):
+            cols = slice(128 * jb, 128 * (jb + 1))
+            if term == 0:
+                rhs, rhs_scale = w1c[b][:, 512 * a : 512 * (a + 1)].bitcast(FP8X4), w1s[b][:, 512 * a : 512 * (a + 1)]
+                v_scale = vs[a][:, cols]
+            else:
+                rhs, rhs_scale = w4w[b][:, a, :].bitcast(FP4X4), w4s[b][:, a, :]
+                v_scale = vs[a][:, cols]
+            nc.tensor.matmul_mx(
+                out=bank[:], lhsT=vw[a][:, cols].bitcast(FP8X4), lhsT_scale=v_scale,
+                rhs=rhs, rhs_scale=rhs_scale, start=(a == 0), stop=(a == KP - 1),
+            )
+
+        def bound(bank, term, jb):
+            nc.scalar.activation(
+                out=tt[term][:, jb, :].rearrange("j (t p) -> j t p", t=4),
+                in_=bank[:].rearrange("j (p t) -> j t p", t=4),
+                func=ACT.Tanh, scale=(1.0 if term == 0 else -1.0),
+            )
+
+        def turn(j0, w):
+            per_bank = 512 // w
+            found = []
+            for t0 in range(0, 4, per_bank):
+                bank = psum.tile([P, 512], F32, name="bank")
+                found.append(bank)
+                for t in range(t0, t0 + per_bank):
+                    for jb in range(j0 // 128, (j0 + w) // 128):
+                        c0 = (t - t0) * w + 128 * jb - j0
+                        for term in range(2):
+                            nc.tensor.matmul(
+                                out=bank[:, c0 : c0 + 128], lhsT=tt[term][:, jb, 128 * t : 128 * (t + 1)], rhs=ident[:],
+                                is_transpose=True, start=(term == 0), stop=(term == 1),
+                            )
+            return found
+
+        def scatter(b, t, src, j0, w):
+            nc.vector.tensor_tensor(
+                out=page[b][t][:].indirect(idx2[:, j0 // 16 : (j0 + w) // 16]),
+                in0=src, in1=factor[b][:, t, j0 : j0 + w], op=ALU.mult,
+            )
+
+        def put_bank(b, bank, t0, j0, w):
+            n = 512 // w
+            nc.scalar.copy(out=hs[b][:, t0 : t0 + n, j0 : j0 + w], in_=bank[:].rearrange("p (t j) -> p t j", j=w))
+            for t in range(t0, t0 + n):
+                scatter(b, t, hs[b][:, t, j0 : j0 + w], j0, w)
+
+        def put_one(b, t, cols, dst, j0, w):
+            nc.scalar.copy(out=dst, in_=cols)
+            scatter(b, t, dst, j0, w)
+
+        def planes(b):
+            return raw[2 - b][:].rearrange("p j c -> p (j c)").bitcast(BF16).rearrange("p (t m) -> p t m", t=4)
+
+        def cast_page(b, t):
+            copy = nc.vector.tensor_copy if (b, t) == (1, 3) else nc.scalar.copy
+            copy(out=planes(b)[:, t, :], in_=page[b][t][:])
+
+        def quant_page(b, mh):
+            cols = slice(512 * mh, 512 * (mh + 1))
+            weave(nc.scalar.copy, pi[b][mh], planes(b)[:, :, cols])
+            quantize(pc[b][:, cols], ps[b][:, cols], pi[b][mh])
+
+        def gather_page(b, dst, j0, w):
+            for t in range(4):
+                nc.vector.tensor_tensor(
+                    out=dst[:, t, :], in0=page[b][t][:].indirect(idx3[:, j0 // 16 : (j0 + w) // 16]),
+                    in1=marks4[b][:, t, j0 : j0 + w], op=ALU.add,
+                )
+
+        def as_f32(woven, w):
+            flat = woven.rearrange("p c t -> p (c t)").bitcast(F32)
+            return flat[:, 0 : 4 * w].rearrange("p (t j) -> p t j", t=4)
+
+        g0 = as_f32(wi12[:], 512)
+        nc.sync.dma_start(idx[:], offs)
+        nc.sync.dma_start(idx2[:], offs2)
+        nc.sync.dma_start(idx3[:], offs3)
+        nc.sync.dma_start(out=gain4[:], in_=gain.rearrange("(b p t) -> p b t", b=RP, t=4))
+        nc.sync.dma_start(out=wgs_rows[:], in_=wgs)
+        load_tab(0)
+        for q in range(4):
+            nc.sync.dma_start(
+                out=tabs[32 * q : 32 * q + 4, :, :].bitcast(I32),
+                in_=tab_scales[:, 4 * q : 4 * q + 4, :].rearrange("a r c -> r a c").bitcast(I32),
+            )
+        load_w1(0, 0)
+        load_w1(0, 1)
+        load_w4s(0)
+        load_tab(1)
+        load_w1(0, 2)
+        load_w4(0)
+        load_tab(2)
+        for t in range(4):
+            load_page(0, t)
+
+        for a in range(KP):
+            nc.vector.tensor_copy(out=vs[a][:], in_=tabs[:, a, :].indirect(idx[:]))
+        for a in range(KP):
+            gather_tab(a, 2 if a == KP - 1 else 1)
+            quant_w1(0, a)
+        bank = psum.tile([P, 512], F32, name="bank")
+        for jb in range(4):
+            nc.tensor.transpose(bank[:, 128 * jb : 128 * (jb + 1)], wgs_rows[:, 128 * jb : 128 * (jb + 1)], ident[:])
+        turned = hs[1][:].rearrange("j jb (t q c) -> j jb t q c", t=4, q=4)
+        for jb in range(4):
+            rows = bank[:, 128 * jb : 128 * (jb + 1)].rearrange("j (c t) -> j t c", t=4)
+            nc.scalar.copy(out=turned[:, jb], in_=rows.unsqueeze(2).to_broadcast([P, 4, 4, 32]))
+        for t in range(4):
+            bank = psum.tile([P, 512], F32, name="bank")
+            for jb in range(4):
+                nc.tensor.transpose(bank[:, 128 * jb : 128 * (jb + 1)], hs[1][:, jb, 128 * t : 128 * (t + 1)], ident[:])
+            nc.scalar.copy(out=hs[0][:, t, :], in_=bank[:])
+            for b in range(RP):
+                nc.gpsimd.tensor_scalar(
+                    out=factor[b][:, t, :], in0=hs[0][:, t, :], scalar1=gain4[:, b, t : t + 1], scalar2=0.0, op0=ALU.mult, op1=ALU.add
+                )
+        banks = [[psum.tile([P, 512], F32, name="bank") for jb in range(4)] for term in range(2)]
+        for a in range(KP - 1):
+            for jb in range(4):
+                for term in range(2):
+                    mm_first(banks[term][jb], term, 0, a, jb)
+        for j0, w in spans(SCATTER_WIDTHS[0]):
+            for jb in range(j0 // 128, (j0 + w) // 128):
+                for term in range(2):
+                    mm_first(banks[term][jb], term, 0, KP - 1, jb)
+                    bound(banks[term][jb], term, jb)
+            found = turn(j0, w)
+            put_bank(0, found[0], 0, j0, w)
+        put_one(0, 2, found[1][:, 0:256], hs[0][:, 2, 256:512], 256, 256)
+
+        load_w4s(1)
+        load_w4(1)
+        for a in range(KP):
+            load_w1(1, a)
+        load_marks(0)
+        nc.sync.dma_start(out=rv4[:], in_=rv.rearrange("(b p t) -> p b t", b=RP, t=4))
+        for t in range(4):
+            load_page(1, t)
+        load_marks(1)
+        with nc.allow_non_contiguous_dma(reason="one value a partition"):
+            nc.sync.dma_start(out=slot8[:], in_=slot.rearrange("(mt p) -> p mt", p=P))
+        for a in range(KP):
+            quant_w1(1, a)
+        put_one(0, 3, found[1][:, 256:512], g0[:, 3, 0:256], 256, 256)
+        banks = [[psum.tile([P, 512], F32, name="bank") for jb in range(4)] for term in range(2)]
+        for jb in range(4):
+            for a in range(KP):
+                mm_first(banks[1][jb], 1, 1, a, jb)
+            bound(banks[1][jb], 1, jb)
+        for jb in range(4):
+            mm_first(banks[0][jb], 0, 1, 0, jb)
+        gather_page(0, g0, 0, NP)
+        for jb in range(4):
+            for a in range(1, KP):
+                mm_first(banks[0][jb], 0, 1, a, jb)
+            bound(banks[0][jb], 0, jb)
+        found = turn(0, S)
+        for t in range(4):
+            put_bank(1, found[t], t, 0, S)
+        for t in range(4):
+            cast_page(0, t)
+        for mh in range(2):
+            quant_page(0, mh)
+        for t in range(4):
+            nc.scalar.activation(out=xp[:, t, :], in_=g0[:, t, :], func=ACT.Copy, scale=rv4[:, 0, t : t + 1])
+        weave(nc.scalar.copy, xi0, xp)
+        quantize(xc[0][:], xs[0][:], xi0)
+        for t in range(4):
+            cast_page(1, t)
+
+        def score_pass(bank, b, pair, j0, w):
+            for i in range(2):
+                m_cols = slice(128 * (2 * pair + i), 128 * (2 * pair + i + 1))
+                nc.tensor.matmul_mx(
+                    out=bank[:, w * i : w * (i + 1)],
+                    lhsT=pc[b][:, m_cols].bitcast(FP8X4), lhsT_scale=ps[b][:, m_cols],
+                    rhs=xc[b][:, j0 : j0 + w].bitcast(FP8X4), rhs_scale=xs[b][:, j0 : j0 + w],
+                    start=(b == 0 and i == 0), stop=(b == RP - 1 and i == 1),
+                )
+
+        def finish(bank, res, pair, j0, w):
+            nc.scalar.activation(out=res, in_=bank[:], func=ACT.Abs)
+            for i in range(2):
+                part = res[:, w * i : w * (i + 1)]
+                mt = 2 * pair + i
+                nc.vector.tensor_scalar(out=part, in0=part, scalar1=slot8[:, mt : mt + 1], scalar2=None, op0=ALU.mult)
+            nc.sync.dma_start(
+                out=out.rearrange("(mt p) j -> p mt j", p=P)[:, 2 * pair : 2 * pair + 2, j0 : j0 + w],
+                in_=res.rearrange("p (i j) -> p i j", j=w),
+            )
+
+        def make_x1(c, host):
+            j0, w = spans(X_WIDTHS[1])[c]
+            g = as_f32(host, w)
+            gather_page(1, g, j0, w)
+            nc.vector.tensor_tensor(
+                out=xi1[c][:].rearrange("p (c i) t -> p c t i", i=4),
+                in0=g.rearrange("p t (c i) -> p c t i", i=4),
+                in1=rv4[:, 1, :].unsqueeze(1).unsqueeze(3).to_broadcast([P, w // 4, 4, 4]),
+                op=ALU.mult,
+            )
+            quantize(xc[1][:, j0 : j0 + w], xs[1][:, j0 : j0 + w], xi1[c][:])
+
+        banks = [[psum.tile([P, 512], F32, name="bank") for pair in range(4)] for c in range(2)]
+        for c in range(2):
+            for pair in range(4):
+                score_pass(banks[c][pair], 0, pair, 256 * c, 256)
+        make_x1(0, xi0)
+        for mh in range(2):
+            quant_page(1, mh)
+        make_x1(1, pi1[:, 1024:3072].rearrange("p (c t) -> p c t", t=4))
+        for c in range(2):
+            for pair in range(4):
+                score_pass(banks[c][pair], 1, pair, 256 * c, 256)
+                finish(banks[c][pair], (tt[1], hs[0])[c][:, pair, :], pair, 256 * c, 256)

@@ -21,7 +21,7 @@ P = 128
 KP = 3
 RP = 2
 SCATTER_WIDTHS = [[128, 128, 256], [512]]
-X_WIDTHS = [[512], [256, 256]]
+X_WIDTHS = [[512], [256,128,128]]
 OUT_WIDTHS = [256, 128, 128]
 
 
@@ -36,10 +36,13 @@ def tile_list_ballot_mark_review_kernel(
     nc = tc.nc
     with ExitStack() as ctx:
         keep = ctx.enter_context(tc.tile_pool(name="keep", bufs=1))
-        psum = ctx.enter_context(tc.psum_pool(name="psum", bufs=8))
+        psum = ctx.enter_context(tc.psum_pool(name="psum", bufs=1))
 
         def tile(name, shape, dtype):
             return keep.tile(shape, dtype, name=name, align_bytes=64)
+
+        def new_bank(n):
+            return psum.tile([P, 512], F32, name="bank%d" % n)
 
         idx = tile("idx", [P, S // 16], U16)
         idx2 = tile("idx2", [P, S // 16], U16)
@@ -120,7 +123,11 @@ def tile_list_ballot_mark_review_kernel(
             nc.vector.quantize_mx(out=codes.bitcast(FP8X4), scales=scales, in_=woven.rearrange("p c t -> p (c t)"))
 
         def quant_w1(b, a):
-            weave(nc.scalar.copy, wi[a], raw[a][:])
+            if (b, a) == (0, 2):
+                weave(nc.scalar.copy, wi[a][:, 0:192, :], raw[a][:, :, 0:192])
+                weave(nc.vector.tensor_copy, wi[a][:, 192:512, :], raw[a][:, :, 192:512])
+            else:
+                weave(nc.scalar.copy, wi[a], raw[a][:])
             if b == 0 or a == 0:
                 quantize(w1c[b][:, 512 * a : 512 * (a + 1)], w1s[b][:, 512 * a : 512 * (a + 1)], wi[a])
             elif a == 2:
@@ -146,28 +153,24 @@ def tile_list_ballot_mark_review_kernel(
                 rhs=rhs, rhs_scale=rhs_scale, start=(a == 0), stop=(a == KP - 1),
             )
 
-        def bound(bank, term, jb):
+        def bound(bank, term, jb, t0=0, t1=4):
             nc.scalar.activation(
-                out=tt[term][:, jb, :].rearrange("j (t p) -> j t p", t=4),
-                in_=bank[:].rearrange("j (p t) -> j t p", t=4),
+                out=tt[term][:, jb, :].rearrange("j (t p) -> j t p", t=4)[:, t0:t1, :],
+                in_=bank[:].rearrange("j (p t) -> j t p", t=4)[:, t0:t1, :],
                 func=ACT.Tanh, scale=(1.0 if term == 0 else -1.0),
             )
 
-        def turn(j0, w):
-            per_bank = 512 // w
-            found = []
-            for t0 in range(0, 4, per_bank):
-                bank = psum.tile([P, 512], F32, name="bank")
-                found.append(bank)
-                for t in range(t0, t0 + per_bank):
-                    for jb in range(j0 // 128, (j0 + w) // 128):
-                        c0 = (t - t0) * w + 128 * jb - j0
-                        for term in range(2):
-                            nc.tensor.matmul(
-                                out=bank[:, c0 : c0 + 128], lhsT=tt[term][:, jb, 128 * t : 128 * (t + 1)], rhs=ident[:],
-                                is_transpose=True, start=(term == 0), stop=(term == 1),
-                            )
-            return found
+        def turn(n, t0, t1, j0, w):
+            bank = new_bank(n)
+            for t in range(t0, t1):
+                for jb in range(j0 // 128, (j0 + w) // 128):
+                    c0 = (t - t0) * w + 128 * jb - j0
+                    for term in range(2):
+                        nc.tensor.matmul(
+                            out=bank[:, c0 : c0 + 128], lhsT=tt[term][:, jb, 128 * t : 128 * (t + 1)], rhs=ident[:],
+                            is_transpose=True, start=(term == 0), stop=(term == 1),
+                        )
+            return bank
 
         def scatter(b, t, src, j0, w):
             nc.vector.tensor_tensor(
@@ -175,10 +178,10 @@ def tile_list_ballot_mark_review_kernel(
                 in0=src, in1=factor[b][:, t, j0 : j0 + w], op=ALU.mult,
             )
 
-        def put_bank(b, bank, t0, j0, w):
-            n = 512 // w
-            nc.scalar.copy(out=hs[b][:, t0 : t0 + n, j0 : j0 + w], in_=bank[:].rearrange("p (t j) -> p t j", j=w))
-            for t in range(t0, t0 + n):
+        def turn_and_put(n, b, t0, t1, j0, w):
+            bank = turn(n, t0, t1, j0, w)
+            nc.scalar.copy(out=hs[b][:, t0:t1, j0 : j0 + w], in_=bank[:, 0 : (t1 - t0) * w].rearrange("p (t j) -> p t j", j=w))
+            for t in range(t0, t1):
                 scatter(b, t, hs[b][:, t, j0 : j0 + w], j0, w)
 
         def put_one(b, t, cols, dst, j0, w):
@@ -189,8 +192,7 @@ def tile_list_ballot_mark_review_kernel(
             return raw[2 - b][:].rearrange("p j c -> p (j c)").bitcast(BF16).rearrange("p (t m) -> p t m", t=4)
 
         def cast_page(b, t):
-            copy = nc.vector.tensor_copy if (b, t) == (1, 3) else nc.scalar.copy
-            copy(out=planes(b)[:, t, :], in_=page[b][t][:])
+            nc.scalar.copy(out=planes(b)[:, t, :], in_=page[b][t][:])
 
         def quant_page(b, mh):
             cols = slice(512 * mh, 512 * (mh + 1))
@@ -210,23 +212,22 @@ def tile_list_ballot_mark_review_kernel(
 
         g0 = as_f32(wi12[:], 512)
         nc.sync.dma_start(idx[:], offs)
-        nc.sync.dma_start(idx2[:], offs2)
-        nc.sync.dma_start(idx3[:], offs3)
-        nc.sync.dma_start(out=gain4[:], in_=gain.rearrange("(b p t) -> p b t", b=RP, t=4))
         nc.sync.dma_start(out=wgs_rows[:], in_=wgs)
         load_tab(0)
+        load_w1(0, 0)
+        nc.sync.dma_start(out=gain4[:], in_=gain.rearrange("(b p t) -> p b t", b=RP, t=4))
         for q in range(4):
             nc.sync.dma_start(
                 out=tabs[32 * q : 32 * q + 4, :, :].bitcast(I32),
                 in_=tab_scales[:, 4 * q : 4 * q + 4, :].rearrange("a r c -> r a c").bitcast(I32),
             )
-        load_w1(0, 0)
         load_w1(0, 1)
-        load_w4s(0)
         load_tab(1)
+        load_w4s(0)
         load_w1(0, 2)
         load_w4(0)
         load_tab(2)
+        nc.sync.dma_start(idx2[:], offs2)
         for t in range(4):
             load_page(0, t)
 
@@ -235,7 +236,7 @@ def tile_list_ballot_mark_review_kernel(
         for a in range(KP):
             gather_tab(a, 2 if a == KP - 1 else 1)
             quant_w1(0, a)
-        bank = psum.tile([P, 512], F32, name="bank")
+        bank = new_bank(0)
         for jb in range(4):
             nc.tensor.transpose(bank[:, 128 * jb : 128 * (jb + 1)], wgs_rows[:, 128 * jb : 128 * (jb + 1)], ident[:])
         turned = hs[1][:].rearrange("j jb (t q c) -> j jb t q c", t=4, q=4)
@@ -243,7 +244,7 @@ def tile_list_ballot_mark_review_kernel(
             rows = bank[:, 128 * jb : 128 * (jb + 1)].rearrange("j (c t) -> j t c", t=4)
             nc.scalar.copy(out=turned[:, jb], in_=rows.unsqueeze(2).to_broadcast([P, 4, 4, 32]))
         for t in range(4):
-            bank = psum.tile([P, 512], F32, name="bank")
+            bank = new_bank(4 + t)
             for jb in range(4):
                 nc.tensor.transpose(bank[:, 128 * jb : 128 * (jb + 1)], hs[1][:, jb, 128 * t : 128 * (t + 1)], ident[:])
             nc.scalar.copy(out=hs[0][:, t, :], in_=bank[:])
@@ -251,24 +252,38 @@ def tile_list_ballot_mark_review_kernel(
                 nc.gpsimd.tensor_scalar(
                     out=factor[b][:, t, :], in0=hs[0][:, t, :], scalar1=gain4[:, b, t : t + 1], scalar2=0.0, op0=ALU.mult, op1=ALU.add
                 )
-        banks = [[psum.tile([P, 512], F32, name="bank") for jb in range(4)] for term in range(2)]
+        banks = [[new_bank(2 * jb + term) for term in range(2)] for jb in range(3)]
         for a in range(KP - 1):
-            for jb in range(4):
+            for jb in range(3):
                 for term in range(2):
-                    mm_first(banks[term][jb], term, 0, a, jb)
-        for j0, w in spans(SCATTER_WIDTHS[0]):
-            for jb in range(j0 // 128, (j0 + w) // 128):
-                for term in range(2):
-                    mm_first(banks[term][jb], term, 0, KP - 1, jb)
-                    bound(banks[term][jb], term, jb)
-            found = turn(j0, w)
-            put_bank(0, found[0], 0, j0, w)
-        put_one(0, 2, found[1][:, 0:256], hs[0][:, 2, 256:512], 256, 256)
+                    mm_first(banks[jb][term], term, 0, a, jb)
+        for term in range(2):
+            mm_first(banks[0][term], term, 0, KP - 1, 0)
+        for half in range(2):
+            for term in range(2):
+                bound(banks[0][term], term, 0, 2 * half, 2 * half + 2)
+            turn_and_put(6 + half, 0, 2 * half, 2 * half + 2, 0, 128)
+        for term in range(2):
+            mm_first(banks[1][term], term, 0, KP - 1, 1)
+            bound(banks[1][term], term, 1)
+        turn_and_put(0, 0, 0, 4, 128, 128)
+        for term in range(2):
+            mm_first(banks[2][term], term, 0, KP - 1, 2)
+            bound(banks[2][term], term, 2)
+        for term in range(2):
+            bank = new_bank((1, 6)[term])
+            for a in range(KP):
+                mm_first(bank, term, 0, a, 3)
+            bound(bank, term, 3)
+        turn_and_put(7, 0, 0, 2, 256, 256)
+        last = turn(2, 2, 4, 256, 256)
+        put_one(0, 2, last[:, 0:256], hs[0][:, 2, 256:512], 256, 256)
 
         load_w4s(1)
         load_w4(1)
         for a in range(KP):
             load_w1(1, a)
+        nc.sync.dma_start(idx3[:], offs3)
         load_marks(0)
         nc.sync.dma_start(out=rv4[:], in_=rv.rearrange("(b p t) -> p b t", b=RP, t=4))
         for t in range(4):
@@ -278,51 +293,64 @@ def tile_list_ballot_mark_review_kernel(
             nc.sync.dma_start(out=slot8[:], in_=slot.rearrange("(mt p) -> p mt", p=P))
         for a in range(KP):
             quant_w1(1, a)
-        put_one(0, 3, found[1][:, 256:512], g0[:, 3, 0:256], 256, 256)
-        banks = [[psum.tile([P, 512], F32, name="bank") for jb in range(4)] for term in range(2)]
+        put_one(0, 3, last[:, 256:512], g0[:, 3, 0:256], 256, 256)
         for jb in range(4):
+            bank = new_bank((3, 4, 5, 0)[jb])
             for a in range(KP):
-                mm_first(banks[1][jb], 1, 1, a, jb)
-            bound(banks[1][jb], 1, jb)
+                mm_first(bank, 1, 1, a, jb)
+            bound(bank, 1, jb)
+        banks = [new_bank(n) for n in (1, 6, 7, 3)]
         for jb in range(4):
-            mm_first(banks[0][jb], 0, 1, 0, jb)
+            mm_first(banks[jb], 0, 1, 0, jb)
         gather_page(0, g0, 0, NP)
-        for jb in range(4):
-            for a in range(1, KP):
-                mm_first(banks[0][jb], 0, 1, a, jb)
-            bound(banks[0][jb], 0, jb)
-        found = turn(0, S)
-        for t in range(4):
-            put_bank(1, found[t], t, 0, S)
+        for half in range(2):
+            for jb in range(2 * half, 2 * half + 2):
+                for a in range(1, KP):
+                    mm_first(banks[jb], 0, 1, a, jb)
+                bound(banks[jb], 0, jb)
+            turn_and_put(4 + half, 1, 0, 2, 256 * half, 256)
+        for t in range(2, 4):
+            turn_and_put(2 * (t - 2), 1, t, t + 1, 0, S)
         for t in range(4):
             cast_page(0, t)
         for mh in range(2):
             quant_page(0, mh)
         for t in range(4):
-            nc.scalar.activation(out=xp[:, t, :], in_=g0[:, t, :], func=ACT.Copy, scale=rv4[:, 0, t : t + 1])
-        weave(nc.scalar.copy, xi0, xp)
+            nc.scalar.activation(out=xp[:, t, 0:256], in_=g0[:, t, 0:256], func=ACT.Copy, scale=rv4[:, 0, t : t + 1])
+        weave(nc.scalar.copy, xi0[:, 0:256, :], xp[:, :, 0:256])
+        nc.vector.tensor_tensor(
+            out=xi0[:, 256:512, :].rearrange("p (c i) t -> p c t i", i=4),
+            in0=g0[:, :, 256:512].rearrange("p t (c i) -> p c t i", i=4),
+            in1=rv4[:, 0, :].unsqueeze(1).unsqueeze(3).to_broadcast([P, 64, 4, 4]),
+            op=ALU.mult,
+        )
         quantize(xc[0][:], xs[0][:], xi0)
         for t in range(4):
             cast_page(1, t)
 
-        def score_pass(bank, b, pair, j0, w):
-            for i in range(2):
-                m_cols = slice(128 * (2 * pair + i), 128 * (2 * pair + i + 1))
+        def score_pass(bank, b, mt0, j0, w):
+            n = 512 // w
+            for i in range(n):
+                m_cols = slice(128 * (mt0 + i), 128 * (mt0 + i + 1))
                 nc.tensor.matmul_mx(
                     out=bank[:, w * i : w * (i + 1)],
                     lhsT=pc[b][:, m_cols].bitcast(FP8X4), lhsT_scale=ps[b][:, m_cols],
                     rhs=xc[b][:, j0 : j0 + w].bitcast(FP8X4), rhs_scale=xs[b][:, j0 : j0 + w],
-                    start=(b == 0 and i == 0), stop=(b == RP - 1 and i == 1),
+                    start=(b == 0 and i == 0), stop=(b == RP - 1 and i == n - 1),
                 )
 
-        def finish(bank, res, pair, j0, w):
+        def finish(bank, res, mt0, j0, w, on_scalar):
+            n = 512 // w
             nc.scalar.activation(out=res, in_=bank[:], func=ACT.Abs)
-            for i in range(2):
+            for i in range(n):
                 part = res[:, w * i : w * (i + 1)]
-                mt = 2 * pair + i
-                nc.vector.tensor_scalar(out=part, in0=part, scalar1=slot8[:, mt : mt + 1], scalar2=None, op0=ALU.mult)
+                s = slot8[:, mt0 + i : mt0 + i + 1]
+                if on_scalar:
+                    nc.scalar.activation(out=part, in_=part, func=ACT.Copy, scale=s)
+                else:
+                    nc.vector.tensor_scalar(out=part, in0=part, scalar1=s, scalar2=None, op0=ALU.mult)
             nc.sync.dma_start(
-                out=out.rearrange("(mt p) j -> p mt j", p=P)[:, 2 * pair : 2 * pair + 2, j0 : j0 + w],
+                out=out.rearrange("(mt p) j -> p mt j", p=P)[:, mt0 : mt0 + n, j0 : j0 + w],
                 in_=res.rearrange("p (i j) -> p i j", j=w),
             )
 
@@ -330,6 +358,17 @@ def tile_list_ballot_mark_review_kernel(
             j0, w = spans(X_WIDTHS[1])[c]
             g = as_f32(host, w)
             gather_page(1, g, j0, w)
+            return g
+
+        def scale_on_scalar(c, g):
+            j0, w = spans(X_WIDTHS[1])[c]
+            for t in range(4):
+                nc.scalar.activation(out=xp[:, t, 0:w], in_=g[:, t, :], func=ACT.Copy, scale=rv4[:, 1, t : t + 1])
+            weave(nc.scalar.copy, xi1[c][:], xp[:, :, 0:w])
+            quantize(xc[1][:, j0 : j0 + w], xs[1][:, j0 : j0 + w], xi1[c][:])
+
+        def scale_on_vector(c, g):
+            j0, w = spans(X_WIDTHS[1])[c]
             nc.vector.tensor_tensor(
                 out=xi1[c][:].rearrange("p (c i) t -> p c t i", i=4),
                 in0=g.rearrange("p t (c i) -> p c t i", i=4),
@@ -338,15 +377,18 @@ def tile_list_ballot_mark_review_kernel(
             )
             quantize(xc[1][:, j0 : j0 + w], xs[1][:, j0 : j0 + w], xi1[c][:])
 
-        banks = [[psum.tile([P, 512], F32, name="bank") for pair in range(4)] for c in range(2)]
-        for c in range(2):
-            for pair in range(4):
-                score_pass(banks[c][pair], 0, pair, 256 * c, 256)
-        make_x1(0, xi0)
+        jobs = [(mt0, j0, w, c) for c, (j0, w) in enumerate(spans(X_WIDTHS[1])) for mt0 in range(0, 8, 512 // w)]
+        banks = [new_bank(n) for n in range(8)]
+        stage = [tile_[:, i, :] for tile_ in (tt[1], hs[0]) for i in range(4)]
+        for bank, (mt0, j0, w, c) in zip(banks, jobs):
+            score_pass(bank, 0, mt0, j0, w)
+        def host(a, b):
+            return pi1[:, a:b].rearrange("p (c t) -> p c t", t=4)
+        scale_on_vector(0, make_x1(0, xi0))
         for mh in range(2):
             quant_page(1, mh)
-        make_x1(1, pi1[:, 1024:3072].rearrange("p (c t) -> p c t", t=4))
-        for c in range(2):
-            for pair in range(4):
-                score_pass(banks[c][pair], 1, pair, 256 * c, 256)
-                finish(banks[c][pair], (tt[1], hs[0])[c][:, pair, :], pair, 256 * c, 256)
+        scale_on_vector(1, make_x1(1, host(2048, 3072)))
+        scale_on_vector(2, make_x1(2, host(3072, 4096)))
+        for k, (bank, res, (mt0, j0, w, c)) in enumerate(zip(banks, stage, jobs)):
+            score_pass(bank, 1, mt0, j0, w)
+            finish(bank, res, mt0, j0, w, k in (0,1,2))

@@ -62,7 +62,7 @@ def tile_list_ballot_mark_review_kernel(
         w1c = [tile("w1c%d" % b, [P, KP * 512], U32) for b in range(RP)]
         w1s = [tile("w1s%d" % b, [P, KP * 512], U8) for b in range(RP)]
         w4w = [tile("w4w%d" % b, [P, KP, 1024], U8) for b in range(RP)]
-        w4s = [tile("w4s%d" % b, [P, KP, 512], U8) for b in range(RP)]
+        w4s = tile("w4s", [P, KP, H], U8)
         wgs_rows = tile("wgs_rows", [P, S], F32)
         factor = [tile("factor%d" % b, [P, 4, S], F32) for b in range(RP)]
         page = [[tile("page%d%d" % (b, t), [P, T2], F32) for t in range(4)] for b in range(RP)]
@@ -77,7 +77,7 @@ def tile_list_ballot_mark_review_kernel(
         pc = [tile("pc%d" % b, [P, T2], U32) for b in range(RP)]
         ps = [tile("ps%d" % b, [P, T2], U8) for b in range(RP)]
         spare = raw[0][:].rearrange("p j c -> p (j c)").bitcast(BF16)
-        xp = spare[:, 0:2048].rearrange("p (t j) -> p t j", t=4)
+        xp = spare[:, 0:1024].rearrange("p (t j) -> p t j", t=4)
         xi0 = spare[:, 2048:4096].rearrange("p (j t) -> p j t", t=4)
         xi1 = [tile("xi1%d" % c, [P, w, 4], BF16) for c, w in enumerate(X_WIDTHS[1])]
         xc = [tile("xc%d" % b, [P, NP], U32) for b in range(RP)]
@@ -85,8 +85,7 @@ def tile_list_ballot_mark_review_kernel(
 
         nc.gpsimd.memset(tabs[:, 0, :].bitcast(I32), 0)
         nc.vector.memset(tabs[:, 1:KP, :].bitcast(I32), 0)
-        for b in range(RP):
-            nc.gpsimd.memset(w4s[b][:].bitcast(I32), 0)
+        nc.gpsimd.memset(w4s[:].bitcast(I32), 0)
         make_identity(nc, ident[:])
 
         def load_tab(a):
@@ -101,13 +100,6 @@ def tile_list_ballot_mark_review_kernel(
                 out=w4w[b][:].bitcast(I32),
                 in_=w4_words[:, :, 1024 * b : 1024 * (b + 1)].rearrange("a p c -> p a c").bitcast(I32),
             )
-
-        def load_w4s(b):
-            for q in range(4):
-                nc.sync.dma_start(
-                    out=w4s[b][32 * q : 32 * q + 4, :, :].bitcast(I32),
-                    in_=w4_scales[:, 4 * q : 4 * q + 4, 512 * b : 512 * (b + 1)].rearrange("a r c -> r a c").bitcast(I32),
-                )
 
         def load_page(b, t):
             rows = page0[512 * b : 512 * (b + 1), :].rearrange("(p t) m -> p t m", t=4)
@@ -146,7 +138,7 @@ def tile_list_ballot_mark_review_kernel(
                 rhs, rhs_scale = w1c[b][:, 512 * a : 512 * (a + 1)].bitcast(FP8X4), w1s[b][:, 512 * a : 512 * (a + 1)]
                 v_scale = vs[a][:, cols]
             else:
-                rhs, rhs_scale = w4w[b][:, a, :].bitcast(FP4X4), w4s[b][:, a, :]
+                rhs, rhs_scale = w4w[b][:, a, :].bitcast(FP4X4), w4s[:, a, 512 * b : 512 * (b + 1)]
                 v_scale = vs[a][:, cols]
             nc.tensor.matmul_mx(
                 out=bank[:], lhsT=vw[a][:, cols].bitcast(FP8X4), lhsT_scale=v_scale,
@@ -178,11 +170,12 @@ def tile_list_ballot_mark_review_kernel(
                 in0=src, in1=factor[b][:, t, j0 : j0 + w], op=ALU.mult,
             )
 
-        def turn_and_put(n, b, t0, t1, j0, w):
+        def turn_and_put(n, b, t0, t1, j0, w, at):
             bank = turn(n, t0, t1, j0, w)
-            nc.scalar.copy(out=hs[b][:, t0:t1, j0 : j0 + w], in_=bank[:, 0 : (t1 - t0) * w].rearrange("p (t j) -> p t j", j=w))
+            dst = hs[b][:].rearrange("p a c -> p (a c)")[:, at : at + (t1 - t0) * w]
+            nc.scalar.copy(out=dst, in_=bank[:, 0 : (t1 - t0) * w])
             for t in range(t0, t1):
-                scatter(b, t, hs[b][:, t, j0 : j0 + w], j0, w)
+                scatter(b, t, dst[:, (t - t0) * w : (t - t0 + 1) * w], j0, w)
 
         def put_one(b, t, cols, dst, j0, w):
             nc.scalar.copy(out=dst, in_=cols)
@@ -214,28 +207,27 @@ def tile_list_ballot_mark_review_kernel(
         nc.sync.dma_start(idx[:], offs)
         nc.sync.dma_start(out=wgs_rows[:], in_=wgs)
         load_tab(0)
-        load_w1(0, 0)
-        nc.sync.dma_start(out=gain4[:], in_=gain.rearrange("(b p t) -> p b t", b=RP, t=4))
         for q in range(4):
             nc.sync.dma_start(
                 out=tabs[32 * q : 32 * q + 4, :, :].bitcast(I32),
                 in_=tab_scales[:, 4 * q : 4 * q + 4, :].rearrange("a r c -> r a c").bitcast(I32),
             )
+        load_w1(0, 0)
+        nc.sync.dma_start(out=gain4[:], in_=gain.rearrange("(b p t) -> p b t", b=RP, t=4))
         load_w1(0, 1)
         load_tab(1)
-        load_w4s(0)
         load_w1(0, 2)
+        for q in range(4):
+            nc.sync.dma_start(
+                out=w4s[32 * q : 32 * q + 4, :, :].bitcast(I32),
+                in_=w4_scales[:, 4 * q : 4 * q + 4, :].rearrange("a r c -> r a c").bitcast(I32),
+            )
         load_w4(0)
         load_tab(2)
         nc.sync.dma_start(idx2[:], offs2)
         for t in range(4):
             load_page(0, t)
 
-        for a in range(KP):
-            nc.vector.tensor_copy(out=vs[a][:], in_=tabs[:, a, :].indirect(idx[:]))
-        for a in range(KP):
-            gather_tab(a, 2 if a == KP - 1 else 1)
-            quant_w1(0, a)
         bank = new_bank(0)
         for jb in range(4):
             nc.tensor.transpose(bank[:, 128 * jb : 128 * (jb + 1)], wgs_rows[:, 128 * jb : 128 * (jb + 1)], ident[:])
@@ -252,6 +244,11 @@ def tile_list_ballot_mark_review_kernel(
                 nc.gpsimd.tensor_scalar(
                     out=factor[b][:, t, :], in0=hs[0][:, t, :], scalar1=gain4[:, b, t : t + 1], scalar2=0.0, op0=ALU.mult, op1=ALU.add
                 )
+        for a in range(KP):
+            nc.vector.tensor_copy(out=vs[a][:], in_=tabs[:, a, :].indirect(idx[:]))
+        for a in range(KP):
+            gather_tab(a, 2 if a == KP - 1 else 1)
+            quant_w1(0, a)
         banks = [[new_bank(2 * jb + term) for term in range(2)] for jb in range(3)]
         for a in range(KP - 1):
             for jb in range(3):
@@ -262,11 +259,11 @@ def tile_list_ballot_mark_review_kernel(
         for half in range(2):
             for term in range(2):
                 bound(banks[0][term], term, 0, 2 * half, 2 * half + 2)
-            turn_and_put(6 + half, 0, 2 * half, 2 * half + 2, 0, 128)
+            turn_and_put(6 + half, 0, 2 * half, 2 * half + 2, 0, 128, 256 * half)
         for term in range(2):
             mm_first(banks[1][term], term, 0, KP - 1, 1)
             bound(banks[1][term], term, 1)
-        turn_and_put(0, 0, 0, 4, 128, 128)
+        turn_and_put(0, 0, 0, 4, 128, 128, 512)
         for term in range(2):
             mm_first(banks[2][term], term, 0, KP - 1, 2)
             bound(banks[2][term], term, 2)
@@ -275,14 +272,13 @@ def tile_list_ballot_mark_review_kernel(
             for a in range(KP):
                 mm_first(bank, term, 0, a, 3)
             bound(bank, term, 3)
-        turn_and_put(7, 0, 0, 2, 256, 256)
+        turn_and_put(7, 0, 0, 2, 256, 256, 1024)
         last = turn(2, 2, 4, 256, 256)
-        put_one(0, 2, last[:, 0:256], hs[0][:, 2, 256:512], 256, 256)
+        put_one(0, 2, last[:, 0:256], hs[0][:, 3, 0:256], 256, 256)
 
-        load_w4s(1)
-        load_w4(1)
         for a in range(KP):
             load_w1(1, a)
+        load_w4(1)
         nc.sync.dma_start(idx3[:], offs3)
         load_marks(0)
         nc.sync.dma_start(out=rv4[:], in_=rv.rearrange("(b p t) -> p b t", b=RP, t=4))
@@ -308,9 +304,9 @@ def tile_list_ballot_mark_review_kernel(
                 for a in range(1, KP):
                     mm_first(banks[jb], 0, 1, a, jb)
                 bound(banks[jb], 0, jb)
-            turn_and_put(4 + half, 1, 0, 2, 256 * half, 256)
+            turn_and_put(4 + half, 1, 0, 2, 256 * half, 256, 512 * half)
         for t in range(2, 4):
-            turn_and_put(2 * (t - 2), 1, t, t + 1, 0, S)
+            turn_and_put(2 * (t - 2), 1, t, t + 1, 0, S, 512 * t)
         for t in range(4):
             cast_page(0, t)
         for mh in range(2):

@@ -18,16 +18,15 @@ ALU = mybir.AluOpType
 ACT = mybir.ActivationFunctionType
 
 P = 128
-KP = 3
-RP = 2
-SCATTER_WIDTHS = [[128, 128, 256], [512]]
-X_WIDTHS = [[512], [256,128,128]]
-OUT_WIDTHS = [256, 128, 128]
+PASS = 512
+K_PASSES = K // PASS
+HALVES = H // PASS
+TERMS = 2
 
-
-def spans(widths):
-    starts = [sum(widths[:i]) for i in range(len(widths))]
-    return list(zip(starts, widths))
+W1_SCALAR_COLUMNS = 192
+PAGE_VECTOR_COLUMNS = 128
+CHUNKS = [(0, 256), (256, 128), (384, 128)]
+BANKS_SCALED_ON_SCALAR = 2
 
 
 def tile_list_ballot_mark_review_kernel(
@@ -42,349 +41,330 @@ def tile_list_ballot_mark_review_kernel(
             return keep.tile(shape, dtype, name=name, align_bytes=64)
 
         def new_bank(n):
-            return psum.tile([P, 512], F32, name="bank%d" % n)
+            return psum.tile([P, PASS], F32, name="bank%d" % n)
+
+        def flat(t3):
+            return t3.rearrange("p a c -> p (a c)")
+
+        def as_woven(flat_bf16):
+            return flat_bf16.rearrange("p (c t) -> p c t", t=4)
+
+        def as_planes(flat_ap):
+            return flat_ap.rearrange("p (t c) -> p t c", t=4)
 
         idx = tile("idx", [P, S // 16], U16)
         idx2 = tile("idx2", [P, S // 16], U16)
         idx3 = tile("idx3", [P, NP // 16], U16)
         ident = tile("ident", [P, P], F32)
-        gain4 = tile("gain4", [P, RP, 4], F32)
-        rv4 = tile("rv4", [P, RP, 4], F32)
-        slot8 = tile("slot8", [P, 8], F32)
-        tabw = [tile("tabw%d" % a, [P, T], U32) for a in range(KP)]
-        tabs = tile("tabs", [P, KP, T], U8)
-        vw = [tile("vw%d" % a, [P, S], U32) for a in range(KP)]
-        vs = [tile("vs%d" % a, [P, S], U8) for a in range(KP)]
-        raw = [tile("raw%d" % a, [P, 4, 512], F32) for a in range(KP)]
-        wi0 = tile("wi0", [P, 512, 4], BF16)
-        wi12 = tile("wi12", [P, 1024, 4], BF16)
-        wi = [wi0[:], wi12[:, 0:512, :], wi12[:, 512:1024, :]]
-        w1c = [tile("w1c%d" % b, [P, KP * 512], U32) for b in range(RP)]
-        w1s = [tile("w1s%d" % b, [P, KP * 512], U8) for b in range(RP)]
-        w4w = [tile("w4w%d" % b, [P, KP, 1024], U8) for b in range(RP)]
-        w4s = tile("w4s", [P, KP, H], U8)
+        gain4 = tile("gain4", [P, HALVES, 4], F32)
+        rv4 = tile("rv4", [P, HALVES, 4], F32)
+        slot8 = tile("slot8", [P, T2 // P], F32)
+        tab_w = [tile("tab_w%d" % a, [P, T], U32) for a in range(K_PASSES)]
+        tab_s = tile("tab_s", [P, K_PASSES, T], U8)
+        v_w = [tile("v_w%d" % a, [P, S], U32) for a in range(K_PASSES)]
+        v_s = [tile("v_s%d" % a, [P, S], U8) for a in range(K_PASSES)]
+        w1_rows = [tile("w1_rows%d" % a, [P, 4, PASS], F32) for a in range(K_PASSES)]
+        w1_woven0 = tile("w1_woven0", [P, PASS, 4], BF16)
+        w1_woven12 = tile("w1_woven12", [P, 2 * PASS, 4], BF16)
+        w1_woven = [w1_woven0[:], w1_woven12[:, 0:PASS, :], w1_woven12[:, PASS : 2 * PASS, :]]
+        w1_w = [tile("w1_w%d" % b, [P, K_PASSES * PASS], U32) for b in range(HALVES)]
+        w1_s = [tile("w1_s%d" % b, [P, K_PASSES * PASS], U8) for b in range(HALVES)]
+        w4_w = [tile("w4_w%d" % b, [P, K_PASSES, 2 * PASS], U8) for b in range(HALVES)]
+        w4_s = tile("w4_s", [P, K_PASSES, H], U8)
         wgs_rows = tile("wgs_rows", [P, S], F32)
-        factor = [tile("factor%d" % b, [P, 4, S], F32) for b in range(RP)]
-        page = [[tile("page%d%d" % (b, t), [P, T2], F32) for t in range(4)] for b in range(RP)]
-        marks4 = [tile("marks%d" % b, [P, 4, NP], F32) for b in range(RP)]
-        tt = [tile("tt%d" % s, [P, 4, 512], F32) for s in range(2)]
-        hs = [tile("hs%d" % b, [P, 4, S], F32) for b in range(RP)]
-        pi1 = tile("pi1", [P, 4096], BF16)
-        pi = [
-            [tt[0][:, 2 * mh : 2 * mh + 2, :].rearrange("p a c -> p (a c)").bitcast(BF16).rearrange("p (c t) -> p c t", t=4) for mh in range(2)],
-            [pi1[:, 2048 * mh : 2048 * (mh + 1)].rearrange("p (c t) -> p c t", t=4) for mh in range(2)],
-        ]
-        pc = [tile("pc%d" % b, [P, T2], U32) for b in range(RP)]
-        ps = [tile("ps%d" % b, [P, T2], U8) for b in range(RP)]
-        spare = raw[0][:].rearrange("p j c -> p (j c)").bitcast(BF16)
-        xp = spare[:, 0:1024].rearrange("p (t j) -> p t j", t=4)
-        xi0 = spare[:, 2048:4096].rearrange("p (j t) -> p j t", t=4)
-        xi1 = [tile("xi1%d" % c, [P, w, 4], BF16) for c, w in enumerate(X_WIDTHS[1])]
-        xc = [tile("xc%d" % b, [P, NP], U32) for b in range(RP)]
-        xs = [tile("xs%d" % b, [P, NP], U8) for b in range(RP)]
+        factor = [tile("factor%d" % b, [P, 4, S], F32) for b in range(HALVES)]
+        page = [[tile("page%d%d" % (b, t), [P, T2], F32) for t in range(4)] for b in range(HALVES)]
+        marks4 = [tile("marks%d" % b, [P, 4, NP], F32) for b in range(HALVES)]
+        bounded = [tile("bounded%d" % term, [P, 4, PASS], F32) for term in range(TERMS)]
+        diff = [tile("diff%d" % b, [P, 4, S], F32) for b in range(HALVES)]
+        page1_woven = tile("page1_woven", [P, 4 * T2], BF16)
+        page_w = [tile("page_w%d" % b, [P, T2], U32) for b in range(HALVES)]
+        page_s = [tile("page_s%d" % b, [P, T2], U8) for b in range(HALVES)]
+        x1_woven = [tile("x1_woven%d" % c, [P, w, 4], BF16) for c, (j0, w) in enumerate(CHUNKS)]
+        x_w = [tile("x_w%d" % b, [P, NP], U32) for b in range(HALVES)]
+        x_s = [tile("x_s%d" % b, [P, NP], U8) for b in range(HALVES)]
 
-        nc.gpsimd.memset(tabs[:, 0, :].bitcast(I32), 0)
-        nc.vector.memset(tabs[:, 1:KP, :].bitcast(I32), 0)
-        nc.gpsimd.memset(w4s[:].bitcast(I32), 0)
+        nc.gpsimd.memset(tab_s[:, 0, :].bitcast(I32), 0)
+        nc.vector.memset(tab_s[:, 1:K_PASSES, :].bitcast(I32), 0)
+        nc.gpsimd.memset(w4_s[:].bitcast(I32), 0)
         make_identity(nc, ident[:])
 
+        def load_scales(dst, src):
+            for q in range(4):
+                rows = src[:, 4 * q : 4 * q + 4, :].rearrange("a i c -> i a c")
+                nc.sync.dma_start(out=dst[32 * q : 32 * q + 4, :, :].bitcast(I32), in_=rows.bitcast(I32))
+
         def load_tab(a):
-            nc.sync.dma_start(out=tabw[a][:].bitcast(I32), in_=tab_words[a].rearrange("p t i -> p (t i)").bitcast(I32))
+            nc.sync.dma_start(out=tab_w[a][:].bitcast(I32), in_=tab_words[a].rearrange("p c i -> p (c i)").bitcast(I32))
 
         def load_w1(b, a):
-            rows = w1[512 * a : 512 * (a + 1), 512 * b : 512 * (b + 1)]
-            nc.sync.dma_start(out=raw[a][:], in_=rows.rearrange("(p j) c -> p j c", j=4))
+            rows = w1[PASS * a : PASS * (a + 1), PASS * b : PASS * (b + 1)]
+            nc.sync.dma_start(out=w1_rows[a][:], in_=rows.rearrange("(p t) c -> p t c", t=4))
 
         def load_w4(b):
-            nc.sync.dma_start(
-                out=w4w[b][:].bitcast(I32),
-                in_=w4_words[:, :, 1024 * b : 1024 * (b + 1)].rearrange("a p c -> p a c").bitcast(I32),
-            )
+            words = w4_words[:, :, 2 * PASS * b : 2 * PASS * (b + 1)].rearrange("a p c -> p a c")
+            nc.sync.dma_start(out=w4_w[b][:].bitcast(I32), in_=words.bitcast(I32))
 
-        def load_page(b, t):
-            rows = page0[512 * b : 512 * (b + 1), :].rearrange("(p t) m -> p t m", t=4)
-            nc.sync.dma_start(out=page[b][t][:], in_=rows[:, t, :])
+        def load_page(b):
+            rows = page0[PASS * b : PASS * (b + 1), :].rearrange("(p t) m -> p t m", t=4)
+            for t in range(4):
+                nc.sync.dma_start(out=page[b][t][:], in_=rows[:, t, :])
 
         def load_marks(b):
-            nc.sync.dma_start(out=marks4[b][:], in_=marks[512 * b : 512 * (b + 1), :].rearrange("(p t) j -> p t j", t=4))
+            nc.sync.dma_start(out=marks4[b][:], in_=marks[PASS * b : PASS * (b + 1), :].rearrange("(p t) j -> p t j", t=4))
 
-        def weave(engine_copy, dst, src):
-            engine_copy(out=dst.rearrange("p (c i) t -> p c t i", i=4), in_=src.rearrange("p t (c i) -> p c t i", i=4))
+        def load_by_row(dst, vec):
+            nc.sync.dma_start(out=dst[:], in_=vec.rearrange("(b p t) -> p b t", b=HALVES, t=4))
 
-        def quantize(codes, scales, woven):
-            nc.vector.quantize_mx(out=codes.bitcast(FP8X4), scales=scales, in_=woven.rearrange("p c t -> p (c t)"))
+        def in_runs(woven, planes, run):
+            return woven.rearrange("p (c i) t -> p c t i", i=run), planes.rearrange("p t (c i) -> p c t i", i=run)
 
-        def quant_w1(b, a):
-            if (b, a) == (0, 2):
-                weave(nc.scalar.copy, wi[a][:, 0:192, :], raw[a][:, :, 0:192])
-                weave(nc.vector.tensor_copy, wi[a][:, 192:512, :], raw[a][:, :, 192:512])
-            else:
-                weave(nc.scalar.copy, wi[a], raw[a][:])
-            if b == 0 or a == 0:
-                quantize(w1c[b][:, 512 * a : 512 * (a + 1)], w1s[b][:, 512 * a : 512 * (a + 1)], wi[a])
-            elif a == 2:
-                quantize(w1c[b][:, 512:1536], w1s[b][:, 512:1536], wi12[:])
+        def weave(copy, woven, planes):
+            dst, src = in_runs(woven, planes, 4)
+            copy(out=dst, in_=src)
 
-        def gather_tab(a, pieces):
-            w = S // pieces
-            for i in range(pieces):
-                nc.vector.tensor_copy(
-                    out=vw[a][:, w * i : w * (i + 1)], in_=tabw[a][:].indirect(idx[:, w * i // 16 : w * (i + 1) // 16])
-                )
+        def quantize(words, scales, woven):
+            nc.vector.quantize_mx(out=words.bitcast(FP8X4), scales=scales, in_=flat(woven))
 
-        def mm_first(bank, term, b, a, jb):
-            cols = slice(128 * jb, 128 * (jb + 1))
+        def product_pass(bank, term, b, a, jb):
+            entries = slice(P * jb, P * (jb + 1))
             if term == 0:
-                rhs, rhs_scale = w1c[b][:, 512 * a : 512 * (a + 1)].bitcast(FP8X4), w1s[b][:, 512 * a : 512 * (a + 1)]
-                v_scale = vs[a][:, cols]
+                cols = slice(PASS * a, PASS * (a + 1))
+                rhs, rhs_scale = w1_w[b][:, cols].bitcast(FP8X4), w1_s[b][:, cols]
             else:
-                rhs, rhs_scale = w4w[b][:, a, :].bitcast(FP4X4), w4s[:, a, 512 * b : 512 * (b + 1)]
-                v_scale = vs[a][:, cols]
+                rhs, rhs_scale = w4_w[b][:, a, :].bitcast(FP4X4), w4_s[:, a, PASS * b : PASS * (b + 1)]
             nc.tensor.matmul_mx(
-                out=bank[:], lhsT=vw[a][:, cols].bitcast(FP8X4), lhsT_scale=v_scale,
-                rhs=rhs, rhs_scale=rhs_scale, start=(a == 0), stop=(a == KP - 1),
+                out=bank[:], lhsT=v_w[a][:, entries].bitcast(FP8X4), lhsT_scale=v_s[a][:, entries],
+                rhs=rhs, rhs_scale=rhs_scale, start=(a == 0), stop=(a == K_PASSES - 1),
             )
 
         def bound(bank, term, jb, t0=0, t1=4):
             nc.scalar.activation(
-                out=tt[term][:, jb, :].rearrange("j (t p) -> j t p", t=4)[:, t0:t1, :],
+                out=as_planes(bounded[term][:, jb, :])[:, t0:t1, :],
                 in_=bank[:].rearrange("j (p t) -> j t p", t=4)[:, t0:t1, :],
-                func=ACT.Tanh, scale=(1.0 if term == 0 else -1.0),
+                func=ACT.Tanh, scale=(1.0, -1.0)[term],
             )
 
         def turn(n, t0, t1, j0, w):
             bank = new_bank(n)
             for t in range(t0, t1):
-                for jb in range(j0 // 128, (j0 + w) // 128):
-                    c0 = (t - t0) * w + 128 * jb - j0
-                    for term in range(2):
+                for jb in range(j0 // P, (j0 + w) // P):
+                    c0 = (t - t0) * w + P * jb - j0
+                    for term in range(TERMS):
                         nc.tensor.matmul(
-                            out=bank[:, c0 : c0 + 128], lhsT=tt[term][:, jb, 128 * t : 128 * (t + 1)], rhs=ident[:],
-                            is_transpose=True, start=(term == 0), stop=(term == 1),
+                            out=bank[:, c0 : c0 + P], lhsT=bounded[term][:, jb, P * t : P * (t + 1)], rhs=ident[:],
+                            is_transpose=True, start=(term == 0), stop=(term == TERMS - 1),
                         )
             return bank
 
-        def scatter(b, t, src, j0, w):
-            nc.vector.tensor_tensor(
-                out=page[b][t][:].indirect(idx2[:, j0 // 16 : (j0 + w) // 16]),
-                in0=src, in1=factor[b][:, t, j0 : j0 + w], op=ALU.mult,
-            )
+        def put(b, t0, t1, j0, w, in_bank, staged):
+            nc.scalar.copy(out=staged, in_=in_bank)
+            for t in range(t0, t1):
+                nc.vector.tensor_tensor(
+                    out=page[b][t][:].indirect(idx2[:, j0 // 16 : (j0 + w) // 16]),
+                    in0=staged[:, (t - t0) * w : (t - t0 + 1) * w], in1=factor[b][:, t, j0 : j0 + w], op=ALU.mult,
+                )
 
         def turn_and_put(n, b, t0, t1, j0, w, at):
-            bank = turn(n, t0, t1, j0, w)
-            dst = hs[b][:].rearrange("p a c -> p (a c)")[:, at : at + (t1 - t0) * w]
-            nc.scalar.copy(out=dst, in_=bank[:, 0 : (t1 - t0) * w])
-            for t in range(t0, t1):
-                scatter(b, t, dst[:, (t - t0) * w : (t - t0 + 1) * w], j0, w)
+            width = (t1 - t0) * w
+            put(b, t0, t1, j0, w, turn(n, t0, t1, j0, w)[:, 0:width], flat(diff[b][:])[:, at : at + width])
 
-        def put_one(b, t, cols, dst, j0, w):
-            nc.scalar.copy(out=dst, in_=cols)
-            scatter(b, t, dst, j0, w)
-
-        def planes(b):
-            return raw[2 - b][:].rearrange("p j c -> p (j c)").bitcast(BF16).rearrange("p (t m) -> p t m", t=4)
-
-        def cast_page(b, t):
-            nc.scalar.copy(out=planes(b)[:, t, :], in_=page[b][t][:])
-
-        def quant_page(b, mh):
-            cols = slice(512 * mh, 512 * (mh + 1))
-            weave(nc.scalar.copy, pi[b][mh], planes(b)[:, :, cols])
-            quantize(pc[b][:, cols], ps[b][:, cols], pi[b][mh])
-
-        def gather_page(b, dst, j0, w):
+        def gather_page(b, picked, j0, w):
             for t in range(4):
                 nc.vector.tensor_tensor(
-                    out=dst[:, t, :], in0=page[b][t][:].indirect(idx3[:, j0 // 16 : (j0 + w) // 16]),
+                    out=picked[:, t, :], in0=page[b][t][:].indirect(idx3[:, j0 // 16 : (j0 + w) // 16]),
                     in1=marks4[b][:, t, j0 : j0 + w], op=ALU.add,
                 )
 
-        def as_f32(woven, w):
-            flat = woven.rearrange("p c t -> p (c t)").bitcast(F32)
-            return flat[:, 0 : 4 * w].rearrange("p (t j) -> p t j", t=4)
-
-        g0 = as_f32(wi12[:], 512)
         nc.sync.dma_start(idx[:], offs)
         nc.sync.dma_start(out=wgs_rows[:], in_=wgs)
         load_tab(0)
-        for q in range(4):
-            nc.sync.dma_start(
-                out=tabs[32 * q : 32 * q + 4, :, :].bitcast(I32),
-                in_=tab_scales[:, 4 * q : 4 * q + 4, :].rearrange("a r c -> r a c").bitcast(I32),
-            )
+        load_scales(tab_s, tab_scales)
         load_w1(0, 0)
-        nc.sync.dma_start(out=gain4[:], in_=gain.rearrange("(b p t) -> p b t", b=RP, t=4))
+        load_by_row(gain4, gain)
+        nc.sync.dma_start(idx2[:], offs2)
         load_w1(0, 1)
         load_tab(1)
         load_w1(0, 2)
-        for q in range(4):
-            nc.sync.dma_start(
-                out=w4s[32 * q : 32 * q + 4, :, :].bitcast(I32),
-                in_=w4_scales[:, 4 * q : 4 * q + 4, :].rearrange("a r c -> r a c").bitcast(I32),
-            )
+        load_scales(w4_s, w4_scales)
         load_w4(0)
         load_tab(2)
-        nc.sync.dma_start(idx2[:], offs2)
-        for t in range(4):
-            load_page(0, t)
+        load_page(0)
 
         bank = new_bank(0)
         for jb in range(4):
-            nc.tensor.transpose(bank[:, 128 * jb : 128 * (jb + 1)], wgs_rows[:, 128 * jb : 128 * (jb + 1)], ident[:])
-        turned = hs[1][:].rearrange("j jb (t q c) -> j jb t q c", t=4, q=4)
+            nc.tensor.transpose(bank[:, P * jb : P * (jb + 1)], wgs_rows[:, P * jb : P * (jb + 1)], ident[:])
+        wgs_dealt = diff[1]
         for jb in range(4):
-            rows = bank[:, 128 * jb : 128 * (jb + 1)].rearrange("j (c t) -> j t c", t=4)
-            nc.scalar.copy(out=turned[:, jb], in_=rows.unsqueeze(2).to_broadcast([P, 4, 4, 32]))
+            by_t = bank[:, P * jb : P * (jb + 1)].rearrange("j (c t) -> j t c", t=4)
+            nc.scalar.copy(
+                out=wgs_dealt[:, jb, :].rearrange("j (t q c) -> j t q c", t=4, q=4),
+                in_=by_t.unsqueeze(2).to_broadcast([P, 4, 4, 32]),
+            )
         for t in range(4):
             bank = new_bank(4 + t)
             for jb in range(4):
-                nc.tensor.transpose(bank[:, 128 * jb : 128 * (jb + 1)], hs[1][:, jb, 128 * t : 128 * (t + 1)], ident[:])
-            nc.scalar.copy(out=hs[0][:, t, :], in_=bank[:])
-            for b in range(RP):
-                nc.gpsimd.tensor_scalar(
-                    out=factor[b][:, t, :], in0=hs[0][:, t, :], scalar1=gain4[:, b, t : t + 1], scalar2=0.0, op0=ALU.mult, op1=ALU.add
-                )
-        for a in range(KP):
-            nc.vector.tensor_copy(out=vs[a][:], in_=tabs[:, a, :].indirect(idx[:]))
-        for a in range(KP):
-            gather_tab(a, 2 if a == KP - 1 else 1)
-            quant_w1(0, a)
-        banks = [[new_bank(2 * jb + term) for term in range(2)] for jb in range(3)]
-        for a in range(KP - 1):
-            for jb in range(3):
-                for term in range(2):
-                    mm_first(banks[jb][term], term, 0, a, jb)
-        for term in range(2):
-            mm_first(banks[0][term], term, 0, KP - 1, 0)
-        for half in range(2):
-            for term in range(2):
-                bound(banks[0][term], term, 0, 2 * half, 2 * half + 2)
-            turn_and_put(6 + half, 0, 2 * half, 2 * half + 2, 0, 128, 256 * half)
-        for term in range(2):
-            mm_first(banks[1][term], term, 0, KP - 1, 1)
-            bound(banks[1][term], term, 1)
-        turn_and_put(0, 0, 0, 4, 128, 128, 512)
-        for term in range(2):
-            mm_first(banks[2][term], term, 0, KP - 1, 2)
-            bound(banks[2][term], term, 2)
-        for term in range(2):
-            bank = new_bank((1, 6)[term])
-            for a in range(KP):
-                mm_first(bank, term, 0, a, 3)
-            bound(bank, term, 3)
-        turn_and_put(7, 0, 0, 2, 256, 256, 1024)
-        last = turn(2, 2, 4, 256, 256)
-        put_one(0, 2, last[:, 0:256], hs[0][:, 3, 0:256], 256, 256)
+                nc.tensor.transpose(bank[:, P * jb : P * (jb + 1)], wgs_dealt[:, jb, P * t : P * (t + 1)], ident[:])
+            for b in range(HALVES):
+                nc.scalar.activation(out=factor[b][:, t, :], in_=bank[:], func=ACT.Copy, scale=gain4[:, b, t : t + 1])
 
-        for a in range(KP):
+        for a in range(K_PASSES):
+            nc.vector.tensor_copy(out=v_s[a][:], in_=tab_s[:, a, :].indirect(idx[:]))
+        for a in range(K_PASSES):
+            piece = S // 2 if a == K_PASSES - 1 else S
+            for j0 in range(0, S, piece):
+                nc.vector.tensor_copy(
+                    out=v_w[a][:, j0 : j0 + piece], in_=tab_w[a][:].indirect(idx[:, j0 // 16 : (j0 + piece) // 16])
+                )
+            cut = W1_SCALAR_COLUMNS if a == K_PASSES - 1 else 0
+            if cut:
+                weave(nc.scalar.copy, w1_woven[a][:, 0:cut, :], w1_rows[a][:, :, 0:cut])
+            weave(nc.vector.tensor_copy, w1_woven[a][:, cut:PASS, :], w1_rows[a][:, :, cut:PASS])
+            quantize(w1_w[0][:, PASS * a : PASS * (a + 1)], w1_s[0][:, PASS * a : PASS * (a + 1)], w1_woven[a])
+
+        y = [[new_bank(TERMS * jb + term) for term in range(TERMS)] for jb in range(3)]
+        for a in range(K_PASSES - 1):
+            for jb in range(3):
+                for term in range(TERMS):
+                    product_pass(y[jb][term], term, 0, a, jb)
+        for term in range(TERMS):
+            product_pass(y[0][term], term, 0, K_PASSES - 1, 0)
+        for t0 in (0, 2):
+            for term in range(TERMS):
+                bound(y[0][term], term, 0, t0, t0 + 2)
+            turn_and_put(6 + t0 // 2, 0, t0, t0 + 2, 0, P, P * t0)
+        for term in range(TERMS):
+            product_pass(y[1][term], term, 0, K_PASSES - 1, 1)
+            bound(y[1][term], term, 1)
+        turn_and_put(0, 0, 0, 4, P, P, 4 * P)
+        for term in range(TERMS):
+            product_pass(y[2][term], term, 0, K_PASSES - 1, 2)
+            bound(y[2][term], term, 2)
+        for term, n in enumerate((1, 6)):
+            bank = new_bank(n)
+            for a in range(K_PASSES):
+                product_pass(bank, term, 0, a, 3)
+            bound(bank, term, 3)
+        turn_and_put(7, 0, 0, 2, 2 * P, 2 * P, 8 * P)
+        last_diff = turn(2, 2, 4, 2 * P, 2 * P)
+        put(0, 2, 3, 2 * P, 2 * P, last_diff[:, 0 : 2 * P], diff[0][:, 3, 0 : 2 * P])
+
+        for a in range(K_PASSES):
             load_w1(1, a)
         load_w4(1)
         nc.sync.dma_start(idx3[:], offs3)
         load_marks(0)
-        nc.sync.dma_start(out=rv4[:], in_=rv.rearrange("(b p t) -> p b t", b=RP, t=4))
-        for t in range(4):
-            load_page(1, t)
+        load_by_row(rv4, rv)
+        load_page(1)
         load_marks(1)
-        with nc.allow_non_contiguous_dma(reason="one value a partition"):
+        with nc.allow_non_contiguous_dma(reason="one value of slot for each partition and tile of 128 rows of out"):
             nc.sync.dma_start(out=slot8[:], in_=slot.rearrange("(mt p) -> p mt", p=P))
-        for a in range(KP):
-            quant_w1(1, a)
-        put_one(0, 3, last[:, 256:512], g0[:, 3, 0:256], 256, 256)
-        for jb in range(4):
-            bank = new_bank((3, 4, 5, 0)[jb])
-            for a in range(KP):
-                mm_first(bank, 1, 1, a, jb)
+
+        weave(nc.scalar.copy, w1_woven[0], w1_rows[0][:])
+        quantize(w1_w[1][:, 0:PASS], w1_s[1][:, 0:PASS], w1_woven[0])
+        for a in range(1, K_PASSES):
+            weave(nc.scalar.copy, w1_woven[a], w1_rows[a][:])
+        quantize(w1_w[1][:, PASS:], w1_s[1][:, PASS:], w1_woven12[:])
+        picked0 = as_planes(flat(w1_woven12[:]).bitcast(F32))
+        put(0, 3, 4, 2 * P, 2 * P, last_diff[:, 2 * P : 4 * P], picked0[:, 3, 0 : 2 * P])
+        for jb, n in enumerate((3, 4, 5, 0)):
+            bank = new_bank(n)
+            for a in range(K_PASSES):
+                product_pass(bank, 1, 1, a, jb)
             bound(bank, 1, jb)
-        banks = [new_bank(n) for n in (1, 6, 7, 3)]
+        y1 = [new_bank(n) for n in (1, 6, 7, 3)]
         for jb in range(4):
-            mm_first(banks[jb], 0, 1, 0, jb)
-        gather_page(0, g0, 0, NP)
-        for half in range(2):
-            for jb in range(2 * half, 2 * half + 2):
-                for a in range(1, KP):
-                    mm_first(banks[jb], 0, 1, a, jb)
-                bound(banks[jb], 0, jb)
-            turn_and_put(4 + half, 1, 0, 2, 256 * half, 256, 512 * half)
-        for t in range(2, 4):
-            turn_and_put(2 * (t - 2), 1, t, t + 1, 0, S, 512 * t)
+            product_pass(y1[jb], 0, 1, 0, jb)
+        gather_page(0, picked0, 0, NP)
+        for pair in range(2):
+            for jb in (2 * pair, 2 * pair + 1):
+                for a in range(1, K_PASSES):
+                    product_pass(y1[jb], 0, 1, a, jb)
+                bound(y1[jb], 0, jb)
+            turn_and_put(4 + pair, 1, 0, 2, 2 * P * pair, 2 * P, 4 * P * pair)
+        for t, n in ((2, 0), (3, 2)):
+            turn_and_put(n, 1, t, t + 1, 0, S, S * t)
+
+        pairs = flat(w1_rows[2][:]).rearrange("m (mb u p) -> m mb u p", u=2, p=P)
+        page0_words = bounded[0]
+        for k in range(4):
+            for mb in (2 * k, 2 * k + 1):
+                bank = new_bank((1, 6, 4, 5)[mb % 4])
+                for t in range(4):
+                    nc.tensor.transpose(bank[:, P * t : P * (t + 1)], page[0][t][:, P * mb : P * (mb + 1)], ident[:])
+                nc.scalar.copy(
+                    out=flat(pairs[:, mb]).bitcast(BF16).rearrange("m (u p e) -> m u p e", u=2, e=2),
+                    in_=bank[:].rearrange("m (u e p) -> m u p e", u=2, e=2),
+                )
+            bank = new_bank((7, 3)[k % 2])
+            for i in range(2):
+                for u in range(2):
+                    nc.tensor.transpose(bank[:, P * (2 * i + u) : P * (2 * i + u + 1)], pairs[:, 2 * k + i, u, :], ident[:])
+            nc.scalar.copy(
+                out=page0_words[:, k, :].rearrange("p (i m u) -> p i m u", i=2, u=2),
+                in_=bank[:].rearrange("p (i u m) -> p i m u", i=2, u=2),
+            )
+        quantize(page_w[0][:], page_s[0][:], as_woven(flat(page0_words[:]).bitcast(BF16)))
+
+        x0_room = flat(w1_rows[0][:]).bitcast(BF16)
+        x0_planes, x0_woven = as_planes(x0_room[:, 0 : 4 * NP]), as_woven(x0_room[:, 4 * NP : 8 * NP])
         for t in range(4):
-            cast_page(0, t)
-        for mh in range(2):
-            quant_page(0, mh)
+            nc.scalar.activation(out=x0_planes[:, t, :], in_=picked0[:, t, :], func=ACT.Copy, scale=rv4[:, 0, t : t + 1])
+        weave(nc.scalar.copy, x0_woven, x0_planes)
+        quantize(x_w[0][:], x_s[0][:], x0_woven)
+
+        page1_planes = as_planes(flat(w1_rows[1][:]).bitcast(BF16))
         for t in range(4):
-            nc.scalar.activation(out=xp[:, t, 0:256], in_=g0[:, t, 0:256], func=ACT.Copy, scale=rv4[:, 0, t : t + 1])
-        weave(nc.scalar.copy, xi0[:, 0:256, :], xp[:, :, 0:256])
-        nc.vector.tensor_tensor(
-            out=xi0[:, 256:512, :].rearrange("p (c i) t -> p c t i", i=4),
-            in0=g0[:, :, 256:512].rearrange("p t (c i) -> p c t i", i=4),
-            in1=rv4[:, 0, :].unsqueeze(1).unsqueeze(3).to_broadcast([P, 64, 4, 4]),
-            op=ALU.mult,
-        )
-        quantize(xc[0][:], xs[0][:], xi0)
-        for t in range(4):
-            cast_page(1, t)
+            nc.scalar.copy(out=page1_planes[:, t, :], in_=page[1][t][:])
+
+        jobs = [(mt0, j0, w) for j0, w in CHUNKS for mt0 in range(0, T2 // P, PASS // w)]
+        e = [new_bank(n) for n in range(len(jobs))]
 
         def score_pass(bank, b, mt0, j0, w):
-            n = 512 // w
-            for i in range(n):
-                m_cols = slice(128 * (mt0 + i), 128 * (mt0 + i + 1))
+            tiles = PASS // w
+            for i in range(tiles):
+                m_cols = slice(P * (mt0 + i), P * (mt0 + i + 1))
                 nc.tensor.matmul_mx(
                     out=bank[:, w * i : w * (i + 1)],
-                    lhsT=pc[b][:, m_cols].bitcast(FP8X4), lhsT_scale=ps[b][:, m_cols],
-                    rhs=xc[b][:, j0 : j0 + w].bitcast(FP8X4), rhs_scale=xs[b][:, j0 : j0 + w],
-                    start=(b == 0 and i == 0), stop=(b == RP - 1 and i == n - 1),
+                    lhsT=page_w[b][:, m_cols].bitcast(FP8X4), lhsT_scale=page_s[b][:, m_cols],
+                    rhs=x_w[b][:, j0 : j0 + w].bitcast(FP8X4), rhs_scale=x_s[b][:, j0 : j0 + w],
+                    start=(b == 0 and i == 0), stop=(b == HALVES - 1 and i == tiles - 1),
                 )
 
-        def finish(bank, res, mt0, j0, w, on_scalar):
-            n = 512 // w
-            nc.scalar.activation(out=res, in_=bank[:], func=ACT.Abs)
-            for i in range(n):
-                part = res[:, w * i : w * (i + 1)]
-                s = slot8[:, mt0 + i : mt0 + i + 1]
-                if on_scalar:
-                    nc.scalar.activation(out=part, in_=part, func=ACT.Copy, scale=s)
+        def make_x1(c, room):
+            j0, w = CHUNKS[c]
+            picked = as_planes(room[:, 0 : 4 * w])
+            gather_page(1, picked, j0, w)
+            dst, src = in_runs(x1_woven[c][:], picked, 2)
+            rv_runs = rv4[:, 1, :].unsqueeze(1).unsqueeze(3).to_broadcast([P, w // 2, 4, 2])
+            nc.vector.tensor_tensor(out=dst, in0=src, in1=rv_runs, op=ALU.mult)
+            quantize(x_w[1][:, j0 : j0 + w], x_s[1][:, j0 : j0 + w], x1_woven[c][:])
+
+        for bank, job in zip(e, jobs):
+            score_pass(bank, 0, *job)
+        make_x1(0, flat(page0_words[:, 2:4, :]))
+        for m0 in (0, PASS):
+            woven = as_woven(page1_woven[:, 4 * m0 : 4 * (m0 + PASS)])
+            cut = PASS - (PAGE_VECTOR_COLUMNS if m0 else 0)
+            weave(nc.scalar.copy, woven[:, 0:cut, :], page1_planes[:, :, m0 : m0 + cut])
+            if cut < PASS:
+                weave(nc.vector.tensor_copy, woven[:, cut:PASS, :], page1_planes[:, :, m0 + cut : m0 + PASS])
+            quantize(page_w[1][:, m0 : m0 + PASS], page_s[1][:, m0 : m0 + PASS], woven)
+        for c, m0 in ((1, 0), (2, PASS)):
+            make_x1(c, page1_woven[:, 4 * m0 : 4 * (m0 + PASS)].bitcast(F32))
+
+        staged_out = [room[:, i, :] for room in (bounded[1], diff[0]) for i in range(4)]
+        out_tiles = out.rearrange("(mt p) j -> p mt j", p=P)
+        for n, (mt0, j0, w) in enumerate(jobs):
+            score_pass(e[n], 1, mt0, j0, w)
+            nc.scalar.activation(out=staged_out[n], in_=e[n][:], func=ACT.Abs)
+            for i in range(PASS // w):
+                part = staged_out[n][:, w * i : w * (i + 1)]
+                slot_col = slot8[:, mt0 + i : mt0 + i + 1]
+                if n < BANKS_SCALED_ON_SCALAR:
+                    nc.scalar.activation(out=part, in_=part, func=ACT.Copy, scale=slot_col)
                 else:
-                    nc.vector.tensor_scalar(out=part, in0=part, scalar1=s, scalar2=None, op0=ALU.mult)
+                    nc.vector.tensor_scalar(out=part, in0=part, scalar1=slot_col, scalar2=None, op0=ALU.mult)
             nc.sync.dma_start(
-                out=out.rearrange("(mt p) j -> p mt j", p=P)[:, mt0 : mt0 + n, j0 : j0 + w],
-                in_=res.rearrange("p (i j) -> p i j", j=w),
+                out=out_tiles[:, mt0 : mt0 + PASS // w, j0 : j0 + w], in_=staged_out[n].rearrange("p (i j) -> p i j", j=w)
             )
-
-        def make_x1(c, host):
-            j0, w = spans(X_WIDTHS[1])[c]
-            g = as_f32(host, w)
-            gather_page(1, g, j0, w)
-            return g
-
-        def scale_on_scalar(c, g):
-            j0, w = spans(X_WIDTHS[1])[c]
-            for t in range(4):
-                nc.scalar.activation(out=xp[:, t, 0:w], in_=g[:, t, :], func=ACT.Copy, scale=rv4[:, 1, t : t + 1])
-            weave(nc.scalar.copy, xi1[c][:], xp[:, :, 0:w])
-            quantize(xc[1][:, j0 : j0 + w], xs[1][:, j0 : j0 + w], xi1[c][:])
-
-        def scale_on_vector(c, g):
-            j0, w = spans(X_WIDTHS[1])[c]
-            nc.vector.tensor_tensor(
-                out=xi1[c][:].rearrange("p (c i) t -> p c t i", i=4),
-                in0=g.rearrange("p t (c i) -> p c t i", i=4),
-                in1=rv4[:, 1, :].unsqueeze(1).unsqueeze(3).to_broadcast([P, w // 4, 4, 4]),
-                op=ALU.mult,
-            )
-            quantize(xc[1][:, j0 : j0 + w], xs[1][:, j0 : j0 + w], xi1[c][:])
-
-        jobs = [(mt0, j0, w, c) for c, (j0, w) in enumerate(spans(X_WIDTHS[1])) for mt0 in range(0, 8, 512 // w)]
-        banks = [new_bank(n) for n in range(8)]
-        stage = [tile_[:, i, :] for tile_ in (tt[1], hs[0]) for i in range(4)]
-        for bank, (mt0, j0, w, c) in zip(banks, jobs):
-            score_pass(bank, 0, mt0, j0, w)
-        def host(a, b):
-            return pi1[:, a:b].rearrange("p (c t) -> p c t", t=4)
-        scale_on_vector(0, make_x1(0, xi0))
-        for mh in range(2):
-            quant_page(1, mh)
-        scale_on_vector(1, make_x1(1, host(2048, 3072)))
-        scale_on_vector(2, make_x1(2, host(3072, 4096)))
-        for k, (bank, res, (mt0, j0, w, c)) in enumerate(zip(banks, stage, jobs)):
-            score_pass(bank, 1, mt0, j0, w)
-            finish(bank, res, mt0, j0, w, k in (0,1,2))

from contextlib import ExitStack

import concourse.mybir as mybir
from concourse.masks import make_identity

K, T, S, H, T2, NP = 1536, 2048, 512, 1024, 1024, 512
FLOPS = 2 * (2 * K * H * S + H * T2 * NP)

F32 = mybir.dt.float32
BF16 = mybir.dt.bfloat16
U32 = mybir.dt.uint32
I32 = mybir.dt.int32
U16 = mybir.dt.uint16
U8 = mybir.dt.uint8
FP8X4 = mybir.dt.float8_e4m3fn_x4
FP4X4 = mybir.dt.float4_e2m1fn_x4
ALU = mybir.AluOpType
ACT = mybir.ActivationFunctionType

P = 128
PASS = 512
K_PASSES = K // PASS
HALVES = H // PASS
TERMS = 2

W1_SCALAR_COLUMNS = 192
PAGE_VECTOR_COLUMNS = 128
CHUNKS = [(0, 256), (256, 128), (384, 128)]
BANKS_SCALED_ON_SCALAR = 2


def tile_list_ballot_mark_review_kernel(
    tc, tab_words, tab_scales, offs, offs2, offs3, w1, w4_words, w4_scales, gain, wgs, page0, marks, rv, slot, out
):
    nc = tc.nc
    with ExitStack() as ctx:
        keep = ctx.enter_context(tc.tile_pool(name="keep", bufs=1))
        psum = ctx.enter_context(tc.psum_pool(name="psum", bufs=1))

        def tile(name, shape, dtype):
            return keep.tile(shape, dtype, name=name, align_bytes=64)

        def new_bank(n):
            return psum.tile([P, PASS], F32, name="bank%d" % n)

        def flat(t3):
            return t3.rearrange("p a c -> p (a c)")

        def as_woven(flat_bf16):
            return flat_bf16.rearrange("p (c t) -> p c t", t=4)

        def as_planes(flat_ap):
            return flat_ap.rearrange("p (t c) -> p t c", t=4)

        idx = tile("idx", [P, S // 16], U16)
        idx2 = tile("idx2", [P, S // 16], U16)
        idx3 = tile("idx3", [P, NP // 16], U16)
        ident = tile("ident", [P, P], F32)
        gain4 = tile("gain4", [P, HALVES, 4], F32)
        rv4 = tile("rv4", [P, HALVES, 4], F32)
        slot8 = tile("slot8", [P, T2 // P], F32)
        tab_w = [tile("tab_w%d" % a, [P, T], U32) for a in range(K_PASSES)]
        tab_s = tile("tab_s", [P, K_PASSES, T], U8)
        v_w = [tile("v_w%d" % a, [P, S], U32) for a in range(K_PASSES)]
        v_s = [tile("v_s%d" % a, [P, S], U8) for a in range(K_PASSES)]
        w1_rows = [tile("w1_rows%d" % a, [P, 4, PASS], F32) for a in range(K_PASSES)]
        w1_woven0 = tile("w1_woven0", [P, PASS, 4], BF16)
        w1_woven12 = tile("w1_woven12", [P, 2 * PASS, 4], BF16)
        w1_woven = [w1_woven0[:], w1_woven12[:, 0:PASS, :], w1_woven12[:, PASS : 2 * PASS, :]]
        w1_w = [tile("w1_w%d" % b, [P, K_PASSES * PASS], U32) for b in range(HALVES)]
        w1_s = [tile("w1_s%d" % b, [P, K_PASSES * PASS], U8) for b in range(HALVES)]
        w4_w = [tile("w4_w%d" % b, [P, K_PASSES, 2 * PASS], U8) for b in range(HALVES)]
        w4_s = tile("w4_s", [P, K_PASSES, H], U8)
        wgs_rows = tile("wgs_rows", [P, S], F32)
        factor = [tile("factor%d" % b, [P, 4, S], F32) for b in range(HALVES)]
        page = [[tile("page%d%d" % (b, t), [P, T2], F32) for t in range(4)] for b in range(HALVES)]
        marks4 = [tile("marks%d" % b, [P, 4, NP], F32) for b in range(HALVES)]
        bounded = [tile("bounded%d" % term, [P, 4, PASS], F32) for term in range(TERMS)]
        diff = [tile("diff%d" % b, [P, 4, S], F32) for b in range(HALVES)]
        page1_woven = tile("page1_woven", [P, 4 * T2], BF16)
        page_w = [tile("page_w%d" % b, [P, T2], U32) for b in range(HALVES)]
        page_s = [tile("page_s%d" % b, [P, T2], U8) for b in range(HALVES)]
        x1_woven = [tile("x1_woven%d" % c, [P, w, 4], BF16) for c, (j0, w) in enumerate(CHUNKS)]
        x_w = [tile("x_w%d" % b, [P, NP], U32) for b in range(HALVES)]
        x_s = [tile("x_s%d" % b, [P, NP], U8) for b in range(HALVES)]

        nc.gpsimd.memset(tab_s[:, 0, :].bitcast(I32), 0)
        nc.vector.memset(tab_s[:, 1:K_PASSES, :].bitcast(I32), 0)
        nc.gpsimd.memset(w4_s[:].bitcast(I32), 0)
        make_identity(nc, ident[:])

        def load_scales(dst, src):
            for q in range(4):
                rows = src[:, 4 * q : 4 * q + 4, :].rearrange("a i c -> i a c")
                nc.sync.dma_start(out=dst[32 * q : 32 * q + 4, :, :].bitcast(I32), in_=rows.bitcast(I32))

        def load_tab(a):
            nc.sync.dma_start(out=tab_w[a][:].bitcast(I32), in_=tab_words[a].rearrange("p c i -> p (c i)").bitcast(I32))

        def load_w1(b, a):
            rows = w1[PASS * a : PASS * (a + 1), PASS * b : PASS * (b + 1)]
            nc.sync.dma_start(out=w1_rows[a][:], in_=rows.rearrange("(p t) c -> p t c", t=4))

        def load_w4(b):
            words = w4_words[:, :, 2 * PASS * b : 2 * PASS * (b + 1)].rearrange("a p c -> p a c")
            nc.sync.dma_start(out=w4_w[b][:].bitcast(I32), in_=words.bitcast(I32))

        def load_page(b):
            rows = page0[PASS * b : PASS * (b + 1), :].rearrange("(p t) m -> p t m", t=4)
            for t in range(4):
                nc.sync.dma_start(out=page[b][t][:], in_=rows[:, t, :])

        def load_marks(b):
            nc.sync.dma_start(out=marks4[b][:], in_=marks[PASS * b : PASS * (b + 1), :].rearrange("(p t) j -> p t j", t=4))

        def load_by_row(dst, vec):
            nc.sync.dma_start(out=dst[:], in_=vec.rearrange("(b p t) -> p b t", b=HALVES, t=4))

        def in_runs(woven, planes, run):
            return woven.rearrange("p (c i) t -> p c t i", i=run), planes.rearrange("p t (c i) -> p c t i", i=run)

        def weave(copy, woven, planes):
            dst, src = in_runs(woven, planes, 4)
            copy(out=dst, in_=src)

        def quantize(words, scales, woven):
            nc.vector.quantize_mx(out=words.bitcast(FP8X4), scales=scales, in_=flat(woven))

        def product_pass(bank, term, b, a, jb):
            entries = slice(P * jb, P * (jb + 1))
            if term == 0:
                cols = slice(PASS * a, PASS * (a + 1))
                rhs, rhs_scale = w1_w[b][:, cols].bitcast(FP8X4), w1_s[b][:, cols]
            else:
                rhs, rhs_scale = w4_w[b][:, a, :].bitcast(FP4X4), w4_s[:, a, PASS * b : PASS * (b + 1)]
            nc.tensor.matmul_mx(
                out=bank[:], lhsT=v_w[a][:, entries].bitcast(FP8X4), lhsT_scale=v_s[a][:, entries],
                rhs=rhs, rhs_scale=rhs_scale, start=(a == 0), stop=(a == K_PASSES - 1),
            )

        def bound(bank, term, jb, t0=0, t1=4):
            nc.scalar.activation(
                out=as_planes(bounded[term][:, jb, :])[:, t0:t1, :],
                in_=bank[:].rearrange("j (p t) -> j t p", t=4)[:, t0:t1, :],
                func=ACT.Tanh, scale=(1.0, -1.0)[term],
            )

        def turn(n, t0, t1, j0, w):
            bank = new_bank(n)
            for t in range(t0, t1):
                for jb in range(j0 // P, (j0 + w) // P):
                    c0 = (t - t0) * w + P * jb - j0
                    for term in range(TERMS):
                        nc.tensor.matmul(
                            out=bank[:, c0 : c0 + P], lhsT=bounded[term][:, jb, P * t : P * (t + 1)], rhs=ident[:],
                            is_transpose=True, start=(term == 0), stop=(term == TERMS - 1),
                        )
            return bank

        def put(b, t0, t1, j0, w, in_bank, staged):
            nc.scalar.copy(out=staged, in_=in_bank)
            for t in range(t0, t1):
                nc.vector.tensor_tensor(
                    out=page[b][t][:].indirect(idx2[:, j0 // 16 : (j0 + w) // 16]),
                    in0=staged[:, (t - t0) * w : (t - t0 + 1) * w], in1=factor[b][:, t, j0 : j0 + w], op=ALU.mult,
                )

        def turn_and_put(n, b, t0, t1, j0, w, at):
            width = (t1 - t0) * w
            put(b, t0, t1, j0, w, turn(n, t0, t1, j0, w)[:, 0:width], flat(diff[b][:])[:, at : at + width])

        def gather_page(b, picked, j0, w):
            for t in range(4):
                nc.vector.tensor_tensor(
                    out=picked[:, t, :], in0=page[b][t][:].indirect(idx3[:, j0 // 16 : (j0 + w) // 16]),
                    in1=marks4[b][:, t, j0 : j0 + w], op=ALU.add,
                )

        nc.sync.dma_start(idx[:], offs)
        nc.sync.dma_start(out=wgs_rows[:], in_=wgs)
        load_tab(0)
        load_scales(tab_s, tab_scales)
        load_w1(0, 0)
        load_by_row(gain4, gain)
        nc.sync.dma_start(idx2[:], offs2)
        load_w1(0, 1)
        load_tab(1)
        load_w1(0, 2)
        load_scales(w4_s, w4_scales)
        load_w4(0)
        load_tab(2)
        load_page(0)

        bank = new_bank(0)
        for jb in range(4):
            nc.tensor.transpose(bank[:, P * jb : P * (jb + 1)], wgs_rows[:, P * jb : P * (jb + 1)], ident[:])
        wgs_dealt = diff[1]
        for jb in range(4):
            by_t = bank[:, P * jb : P * (jb + 1)].rearrange("j (c t) -> j t c", t=4)
            nc.scalar.copy(
                out=wgs_dealt[:, jb, :].rearrange("j (t q c) -> j t q c", t=4, q=4),
                in_=by_t.unsqueeze(2).to_broadcast([P, 4, 4, 32]),
            )
        for t in range(4):
            bank = new_bank(4 + t)
            for jb in range(4):
                nc.tensor.transpose(bank[:, P * jb : P * (jb + 1)], wgs_dealt[:, jb, P * t : P * (t + 1)], ident[:])
            for b in range(HALVES):
                nc.scalar.activation(out=factor[b][:, t, :], in_=bank[:], func=ACT.Copy, scale=gain4[:, b, t : t + 1])

        for a in range(K_PASSES):
            nc.vector.tensor_copy(out=v_s[a][:], in_=tab_s[:, a, :].indirect(idx[:]))
        for a in range(K_PASSES):
            piece = S // 2 if a == K_PASSES - 1 else S
            for j0 in range(0, S, piece):
                nc.vector.tensor_copy(
                    out=v_w[a][:, j0 : j0 + piece], in_=tab_w[a][:].indirect(idx[:, j0 // 16 : (j0 + piece) // 16])
                )
            cut = W1_SCALAR_COLUMNS if a == K_PASSES - 1 else 0
            if cut:
                weave(nc.scalar.copy, w1_woven[a][:, 0:cut, :], w1_rows[a][:, :, 0:cut])
            weave(nc.vector.tensor_copy, w1_woven[a][:, cut:PASS, :], w1_rows[a][:, :, cut:PASS])
            quantize(w1_w[0][:, PASS * a : PASS * (a + 1)], w1_s[0][:, PASS * a : PASS * (a + 1)], w1_woven[a])

        y = [[new_bank(TERMS * jb + term) for term in range(TERMS)] for jb in range(3)]
        for a in range(K_PASSES - 1):
            for jb in range(3):
                for term in range(TERMS):
                    product_pass(y[jb][term], term, 0, a, jb)
        for term in range(TERMS):
            product_pass(y[0][term], term, 0, K_PASSES - 1, 0)
        for t0 in (0, 2):
            for term in range(TERMS):
                bound(y[0][term], term, 0, t0, t0 + 2)
            turn_and_put(6 + t0 // 2, 0, t0, t0 + 2, 0, P, P * t0)
        for term in range(TERMS):
            product_pass(y[1][term], term, 0, K_PASSES - 1, 1)
            bound(y[1][term], term, 1)
        turn_and_put(0, 0, 0, 4, P, P, 4 * P)
        for term in range(TERMS):
            product_pass(y[2][term], term, 0, K_PASSES - 1, 2)
            bound(y[2][term], term, 2)
        for term, n in enumerate((1, 6)):
            bank = new_bank(n)
            for a in range(K_PASSES):
                product_pass(bank, term, 0, a, 3)
            bound(bank, term, 3)
        turn_and_put(7, 0, 0, 2, 2 * P, 2 * P, 8 * P)
        last_diff = turn(2, 2, 4, 2 * P, 2 * P)
        put(0, 2, 3, 2 * P, 2 * P, last_diff[:, 0 : 2 * P], diff[0][:, 3, 0 : 2 * P])

        for a in range(K_PASSES):
            load_w1(1, a)
        load_w4(1)
        nc.sync.dma_start(idx3[:], offs3)
        load_marks(0)
        load_by_row(rv4, rv)
        load_page(1)
        load_marks(1)
        with nc.allow_non_contiguous_dma(reason="one value of slot for each partition and tile of 128 rows of out"):
            nc.sync.dma_start(out=slot8[:], in_=slot.rearrange("(mt p) -> p mt", p=P))

        weave(nc.scalar.copy, w1_woven[0], w1_rows[0][:])
        quantize(w1_w[1][:, 0:PASS], w1_s[1][:, 0:PASS], w1_woven[0])
        for a in range(1, K_PASSES):
            weave(nc.scalar.copy, w1_woven[a], w1_rows[a][:])
        quantize(w1_w[1][:, PASS:], w1_s[1][:, PASS:], w1_woven12[:])
        picked0 = as_planes(flat(w1_woven12[:]).bitcast(F32))
        put(0, 3, 4, 2 * P, 2 * P, last_diff[:, 2 * P : 4 * P], picked0[:, 3, 0 : 2 * P])
        for jb, n in enumerate((3, 4, 5, 0)):
            bank = new_bank(n)
            for a in range(K_PASSES):
                product_pass(bank, 1, 1, a, jb)
            bound(bank, 1, jb)
        y1 = [new_bank(n) for n in (1, 6, 7, 3)]
        for jb in range(4):
            product_pass(y1[jb], 0, 1, 0, jb)
        gather_page(0, picked0, 0, NP)
        for pair in range(2):
            for jb in (2 * pair, 2 * pair + 1):
                for a in range(1, K_PASSES):
                    product_pass(y1[jb], 0, 1, a, jb)
                bound(y1[jb], 0, jb)
            turn_and_put(4 + pair, 1, 0, 2, 2 * P * pair, 2 * P, 4 * P * pair)
        for t, n in ((2, 0), (3, 2)):
            turn_and_put(n, 1, t, t + 1, 0, S, S * t)

        pairs = flat(w1_rows[2][:]).rearrange("m (mb u p) -> m mb u p", u=2, p=P)
        page0_words = bounded[0]
        for k in range(4):
            for mb in (2 * k, 2 * k + 1):
                bank = new_bank((1, 6, 4, 5)[mb % 4])
                for t in range(4):
                    nc.tensor.transpose(bank[:, P * t : P * (t + 1)], page[0][t][:, P * mb : P * (mb + 1)], ident[:])
                nc.scalar.copy(
                    out=flat(pairs[:, mb]).bitcast(BF16).rearrange("m (u p e) -> m u p e", u=2, e=2),
                    in_=bank[:].rearrange("m (u e p) -> m u p e", u=2, e=2),
                )
            bank = new_bank((7, 3)[k % 2])
            for i in range(2):
                for u in range(2):
                    nc.tensor.transpose(bank[:, P * (2 * i + u) : P * (2 * i + u + 1)], pairs[:, 2 * k + i, u, :], ident[:])
            nc.scalar.copy(
                out=page0_words[:, k, :].rearrange("p (i m u) -> p i m u", i=2, u=2),
                in_=bank[:].rearrange("p (i u m) -> p i m u", i=2, u=2),
            )
        quantize(page_w[0][:], page_s[0][:], as_woven(flat(page0_words[:]).bitcast(BF16)))

        x0_room = flat(w1_rows[0][:]).bitcast(BF16)
        x0_planes, x0_woven = as_planes(x0_room[:, 0 : 4 * NP]), as_woven(x0_room[:, 4 * NP : 8 * NP])
        for t in range(4):
            nc.scalar.activation(out=x0_planes[:, t, :], in_=picked0[:, t, :], func=ACT.Copy, scale=rv4[:, 0, t : t + 1])
        weave(nc.scalar.copy, x0_woven, x0_planes)
        quantize(x_w[0][:], x_s[0][:], x0_woven)

        page1_planes = as_planes(flat(w1_rows[1][:]).bitcast(BF16))
        for t in range(4):
            nc.scalar.copy(out=page1_planes[:, t, :], in_=page[1][t][:])

        jobs = [(mt0, j0, w) for j0, w in CHUNKS for mt0 in range(0, T2 // P, PASS // w)]
        e = [new_bank(n) for n in range(len(jobs))]

        def score_pass(bank, b, mt0, j0, w):
            tiles = PASS // w
            for i in range(tiles):
                m_cols = slice(P * (mt0 + i), P * (mt0 + i + 1))
                nc.tensor.matmul_mx(
                    out=bank[:, w * i : w * (i + 1)],
                    lhsT=page_w[b][:, m_cols].bitcast(FP8X4), lhsT_scale=page_s[b][:, m_cols],
                    rhs=x_w[b][:, j0 : j0 + w].bitcast(FP8X4), rhs_scale=x_s[b][:, j0 : j0 + w],
                    start=(b == 0 and i == 0), stop=(b == HALVES - 1 and i == tiles - 1),
                )

        def make_x1(c, room):
            j0, w = CHUNKS[c]
            picked = as_planes(room[:, 0 : 4 * w])
            gather_page(1, picked, j0, w)
            dst, src = in_runs(x1_woven[c][:], picked, 2)
            rv_runs = rv4[:, 1, :].unsqueeze(1).unsqueeze(3).to_broadcast([P, w // 2, 4, 2])
            nc.vector.tensor_tensor(out=dst, in0=src, in1=rv_runs, op=ALU.mult)
            quantize(x_w[1][:, j0 : j0 + w], x_s[1][:, j0 : j0 + w], x1_woven[c][:])

        for bank, job in zip(e, jobs):
            score_pass(bank, 0, *job)
        make_x1(0, flat(page0_words[:, 2:4, :]))
        for m0 in (0, PASS):
            woven = as_woven(page1_woven[:, 4 * m0 : 4 * (m0 + PASS)])
            cut = PASS - (PAGE_VECTOR_COLUMNS if m0 else 0)
            weave(nc.scalar.copy, woven[:, 0:cut, :], page1_planes[:, :, m0 : m0 + cut])
            if cut < PASS:
                weave(nc.vector.tensor_copy, woven[:, cut:PASS, :], page1_planes[:, :, m0 + cut : m0 + PASS])
            quantize(page_w[1][:, m0 : m0 + PASS], page_s[1][:, m0 : m0 + PASS], woven)
        for c, m0 in ((1, 0), (2, PASS)):
            make_x1(c, page1_woven[:, 4 * m0 : 4 * (m0 + PASS)].bitcast(F32))

        staged_out = [room[:, i, :] for room in (bounded[1], diff[0]) for i in range(4)]
        out_tiles = out.rearrange("(mt p) j -> p mt j", p=P)
        for n, (mt0, j0, w) in enumerate(jobs):
            score_pass(e[n], 1, mt0, j0, w)
            nc.scalar.activation(out=staged_out[n], in_=e[n][:], func=ACT.Abs)
            for i in range(PASS // w):
                part = staged_out[n][:, w * i : w * (i + 1)]
                slot_col = slot8[:, mt0 + i : mt0 + i + 1]
                if n < BANKS_SCALED_ON_SCALAR:
                    nc.scalar.activation(out=part, in_=part, func=ACT.Copy, scale=slot_col)
                else:
                    nc.vector.tensor_scalar(out=part, in0=part, scalar1=slot_col, scalar2=None, op0=ALU.mult)
            nc.sync.dma_start(
                out=out_tiles[:, mt0 : mt0 + PASS // w, j0 : j0 + w], in_=staged_out[n].rearrange("p (i j) -> p i j", j=w)
            )
